import numpy as np, ml_dtypes
CORES = [10,34,74,98]
N = 4
import mx_ref
BF = ml_dtypes.bfloat16
def gentries(a):
    return np.ascontiguousarray(a.reshape(8, 16, -1).transpose(0, 2, 1)).reshape(8, -1)
def gtable(e):
    e = np.asarray(e); return np.ascontiguousarray(e.reshape(8, -1, 16).transpose(0, 2, 1)).reshape(128, -1).astype(np.int32)
def gcols(t, e):
    v = np.concatenate([t.reshape(8, 16, -1, 4), np.zeros((8, 16, 1, 4), BF)], axis=2)
    return np.ascontiguousarray(np.stack([v[g][:, e[g]] for g in range(8)])).reshape(128, -1)
def tile(rs):
    return np.stack(rs, axis=2).reshape(128, -1).astype(BF)
def pick(q, e):
    c = np.concatenate([q[0].reshape(128, -1, 4), np.zeros((128, 1, 4), np.uint8)], axis=1); s = np.concatenate([q[1], np.ones((16, 1), np.uint8)], axis=1)
    return (np.ascontiguousarray(c[:, e].reshape(128, -1)), np.ascontiguousarray(s[:, e]))
def join(*qs):
    return (np.concatenate([q[0] for q in qs], axis=1), np.concatenate([q[1] for q in qs], axis=1))
def put(q, e, v):
    c, s = q[0].reshape(128, -1, 4).copy(), q[1].copy(); c[:, e] = v[0].reshape(128, -1, 4); s[:, e] = v[1]
    return (c.reshape(128, -1), s)
def pk(c, s):
    return (np.ascontiguousarray(c), mx_ref.live(s))
def emit(q):
    return q[0], q[1]
def packed(v, rng):
    q = [mx_ref.quantize(np.ascontiguousarray(v[r])) for r in range(N)]
    return np.stack([a for a, b in q]), np.stack([mx_ref.plane(b, rng) for a, b in q])
def values_of_codes():
    e, c = np.zeros((128, 128, 4), np.float32), np.zeros((128, 2, 4), np.uint8)
    e[np.arange(128), np.arange(128), 0] = 1
    c[:127, :, 0] = np.arange(256).reshape(2, 128).T[:127]
    return mx_ref.matmul(mx_ref.quantize(e.reshape(128, 512).astype(BF)), (c.reshape(128, 8), np.full((16, 2), 127, np.uint8))).T.reshape(-1).astype(np.float64)
CODE_VALUE, SCALE_VALUE = values_of_codes(), 2.0 ** (np.arange(256) - 127.0)
def decode(q):
    return (CODE_VALUE[q[0]].reshape(16, 8, -1, 4) * SCALE_VALUE[q[1]][:, None, :, None] + 0.0).reshape(128, -1).astype(np.float32)
def f(rng, *shape):
    return mx_ref.flush((rng.standard_normal(shape, dtype=np.float32) * np.exp2(rng.integers(-2, 3, shape[:-1] + (1,)))).astype(BF))
def wide(rng, *shape, cols=0):
    v = rng.standard_normal(shape, dtype=np.float32) * np.exp2(rng.integers(-12, 13, shape)).astype(np.float32)
    if cols: v *= np.repeat(np.exp2(rng.integers(-cols, cols + 1, shape[:-2] + (1, shape[-1] // 4))) * (rng.random(shape[:-2] + (1, shape[-1] // 4)) > 0.0625), 4, axis=-1).astype(np.float32)
    return mx_ref.flush(v.astype(BF))
C = 416
MASK = [1, 2, 3]
def numbers_of(rng):
    return {"x": np.array(f(rng, N, 128, 4 * C)), "u": np.array(f(rng, N, 128, 512)), "v": np.array(f(rng, N, 128, 512))}
def following(o):
    e = np.zeros_like(o)
    np.put_along_axis(e, o, np.roll(o, -1, axis=-1), axis=-1)
    return e
def rings(rng):
    return following(rng.permuted(np.tile(np.arange(C), (N, 8, 1)), axis=2))
def runs(rng, when, same=False):
    o, go = np.zeros((N, 8, C), np.int64), np.zeros((N, 8, C), bool)
    for r in range(N):
        k = rng.permutation(C)
        for g in range(8):
            p = r ^ MASK[when[g]]
            if p < r: continue
            if not same: k = rng.permutation(C)
            for i, m in ((r, [1, 0, 3, 2]), (p, [2, 0, 3, 1])):
                q = rng.permuted(k.reshape(4, -1), axis=1)[m]
                o[i, g] = np.concatenate([q[:2].T.reshape(-1), q[2:].T.reshape(-1)])
                go[i, g, q[:2].reshape(-1)] = True
    return following(o), go
def stored(e):
    return {"nx": np.stack([gtable(e[r]) for r in range(N)])}
def layers(rng, still=[]):
    w = np.array(f(rng, N, 128, 2048)).reshape(N, 8, 16, 4, 8, 16, 4)
    for i in still:
        w[:, :, i] = 0
        w[:, :, :, :, :, i] = 0
    return w
def weights(rng, w):
    c, s = packed(np.ascontiguousarray(w).reshape(N, 128, 2048), rng)
    return {"wc": c, "ws": s}
def setup_inputs(rng):
    return {**numbers_of(rng), **stored(rings(rng)), **weights(rng, layers(rng))}
def setup_inputs_ties(rng):
    d = numbers_of(rng)
    o = rng.permutation(N)
    k = rng.integers(-1, 2, (N, 8, C)).astype(np.float32)
    k[o[1]] = 1
    x = d["x"].reshape(N, 8, 16, C, 4)
    x[:, :, 0] = 0
    x[:, :, 0, :, 0] = k.astype(BF)
    c = np.ones(N, np.float32)
    c[o[0]] = 0
    c[o[2]] = -1
    u = d["u"].reshape(N, 128, 128, 4)
    u[:, :, ::16] = 0
    for h in range(0, 128, 16): u[:, h, h, 0] = c.astype(BF)
    e, i = rings(rng), np.arange(C)
    for r in range(N):
        p, h = r ^ MASK[0], rng.permutation(8)
        if p < r: continue
        e[p, h[0]] = e[r, h[0]]
        e[p, h[1]] = np.argsort(e[r, h[1]])
        e[r, h[2]], e[p, h[2]] = (i + 1) % C, (i - 1) % C
        e[r, h[3]] = e[p, h[3]] = (i + 1) % C
    w = layers(rng)
    w[:, :, :, :, :, :8] = 0
    return {"x": x.reshape(N, 128, 4 * C), "u": u.reshape(N, 128, 512), "v": d["v"], **stored(e), **weights(rng, w)}
def setup_inputs_near(rng):
    d = numbers_of(rng)
    o = rng.permutation(N) % 4
    k = np.where(o % 2 == 0, 1.0, 2.0 ** -30)
    x = np.zeros((N, 8, 16, C, 4))
    s = rng.integers(-1, 2, (N, 8, C)) * k[:, None, None]
    x[:, :, 0, :, 0] = 1.125 * s
    x[:, :, 1, :, 0] = -1.25 * s
    x[:, :, 8, :, 0] = rng.integers(-1, 2, (N, 8, C)) * 2.0 ** -27
    x[:, :, 8, :, 1] = 2.0 ** -27
    x[:, :, 9:] = (1.0 + rng.integers(0, 128, (N, 8, 7, C, 4)) * 2.0 ** -7) * 2.0 ** -27 * rng.choice([-1.0, 1.0], (N, 8, 7, C, 4))
    w = layers(rng, list(range(9)))
    for r in range(N):
        if o[r] % 2 == 1: x[r, :, 7, :, 0] = 2.0 ** -26
        if o[r] == 3:
            x[r, :, :2] = 0
            x[r, :, 7, :, 0] = 2.0 ** -27
            for g in range(8):
                w[r, g, 8, 0, g, 0, 0] = 2.0 ** -10
                w[r, g, 8, 0, g, 0, 1] = 2.0 ** -8
                w[r, g, 8, 0, g, 1, 0] = -2.0 ** -10
                w[r, g, 8, 0, g, 1, 1] = -1.125 * 2.0 ** -8
        else:
            at = [0, C - 1, int(rng.integers(C)), int(rng.integers(C))]
            for g, j in zip(rng.permutation(8)[:4], at): x[r, g, 0, j, 0] = 2.0 ** 30 * rng.choice([-1.0, 1.0])
    u = d["u"].reshape(N, 128, 128, 4)
    u[:, :, ::16] = 0
    for h in range(0, 128, 16):
        u[:, h, h, 0] = (1.125 * k).astype(np.float32).astype(BF)
        u[:, h + 1, h, 0] = k.astype(np.float32).astype(BF)
    return {"x": x.astype(np.float32).reshape(N, 128, 4 * C).astype(BF), "u": u.reshape(N, 128, 512), "v": d["v"], **stored(rings(rng)), **weights(rng, w)}
def setup_inputs_runs(rng):
    d = numbers_of(rng)
    o = rng.permutation(8)
    when = np.zeros(8, np.int64)
    when[o[4:6]] = 1
    when[o[6:]] = 2
    e, go = runs(rng, when)
    low = -rng.integers(0, 2, (N, 8, C))
    t = np.where(go, 1, low)
    for r in range(N):
        h = rng.permutation(o[:4])
        t[r, h[0]] = 1
        t[r, h[1]] = low[r, h[1]]
    for g in o[4:]:
        for i in range(when[g]): t[:, g] = np.take_along_axis(t[:, g], e[:, g], axis=1)
    x = (1.0 + (2 * rng.integers(0, 64, (N, 16, 8, C, 4)) + 1) * 2.0 ** -7) * np.exp2(-rng.integers(0, 7, (N, 16, 8, C, 4)).astype(np.float64)) * rng.choice([-1.0, 1.0], (N, 16, 8, C, 4))
    c = rng.choice([-1.0, 1.0], (N, 16, 1))
    k = np.exp2(when - 8.0)[:, None]
    x[:, :, 0, :, 0] = np.where(rng.random((N, 16, C)) < 0.5, 1.96875, 1.875) * 2.0 ** 8 * c
    x[:, :, 3, :, 0] = 1.875 * 2.0 ** 7
    x[:, ::2, 1, :, 0] = (8 + t) * k
    x[:, ::2, 2, :, 0] = 8 * k
    u = d["u"].reshape(N, 128, 128, 4)
    u[:, :, ::16] = 0
    for h in range(0, 128, 16):
        u[:, h + 1, h, 0] = 1
        u[:, h + 2, h, 0] = -1
    w = layers(rng, [0, 3, 8, 11])
    for g in range(8):
        for i in (0, 1):
            w[:, g, 8 * i + 3, 0, g, 8 * i, 0] = (64 * c[:, 2 * g + i, 0]).astype(np.float32).astype(BF)
            w[:, g, 8 * i + 3, 0, g, 8 * i + 3, 0] = 32
    for g in o[4:]:
        x[:, 2 * g, 4, :, 0] = -1.0
        x[:, 2 * g, 5, :, 0] = 1.0 - when[g]
        u[:, 16 * g + 4, 16 * g, 0] = 1
        for i in (1, 2, 4, 5): w[:, :, :, :, g, i] = 0
        w[:, g, 4, 0, g, 4, 0] = -32
        w[:, g, 5, 0, g, 4, 0] = 64
        w[:, g, 5, 0, g, 5, 0] = -32
    return {"x": x.astype(np.float32).reshape(N, 128, 4 * C).astype(BF), "u": u.reshape(N, 128, 512), "v": d["v"], **stored(e), **weights(rng, w)}
def setup_inputs_ends(rng):
    d = numbers_of(rng)
    e, go = runs(rng, np.zeros(8, np.int64), True)
    o = rng.permutation(N) % 4
    s = go[:, 0] * 2.0 - 1.0
    small = (1.0 + 0.125 * rng.integers(0, 8, (N, 8, 16, C, 4))) * 2.0 ** -20
    x = (0.9 + 0.1 * rng.random((N, 8, 16, C, 4))) * 2.0 ** 30
    u = d["u"].astype(np.float32).reshape(N, 128, 128, 4)
    v = np.zeros((N, 128, 512), np.float32)
    w = np.zeros((N, 128, 4, 128, 4), np.float32)
    i = np.arange(128)
    for r in range(N):
        if o[r] == 0: x[r] *= s[r][:, None]
        if o[r] == 1: x[r] *= -1
        if o[r] == 2: x[r] *= rng.choice([-1.0, 1.0], (8, 1, C, 1))
        if o[r] == 3: x[r] = small[r] * s[r][:, None]
        x[r, 7, 8:] = small[r, 7, 8:] * rng.choice([-1.0, 1.0], (8, C, 4))
        c = np.array([0.0, 1, 1, 1, -1, -1, -1, -1])[rng.permutation(8)][None, :, None]
        if o[r] < 3: u[r, :, ::16] = c * (0.9 + 0.1 * rng.random((128, 8, 4))) * 2.0 ** 30
        else: u[r, :, ::16] = c * (1.0 + 0.125 * rng.integers(0, 8, (128, 8, 4))) * 2.0 ** -30
        if o[r] < 2: v[r] = (0.9 + 0.1 * rng.random((128, 512))) * 2.0 ** 30
        else: v[r] = (1.0 + 0.125 * rng.integers(0, 8, (128, 512))) * 2.0 ** -30
        v[r] *= rng.choice([-1.0, 1.0], (128, 512))
        k = np.full(128, 32.0)
        if o[r] == 3: k = np.where(i < 120, 2.0 ** -8, 2.0 ** 8)
        for b in range(4): w[r, i, b, i, b] = k
    return {"x": x.astype(np.float32).reshape(N, 128, 4 * C).astype(BF), "u": u.reshape(N, 128, 512).astype(BF), "v": v.astype(BF), **stored(e), **weights(rng, w.astype(BF))}
def setup_inputs_spread(rng):
    d = setup_inputs(rng)
    d["x"] = wide(rng, N, 128, 4 * C, cols=6)
    return d
def check_inputs(d):
    b = []
    for k in ("x", "u", "v"):
        a = np.abs(d[k].astype(np.float32))
        if not (np.isfinite(a).all() and ((a == 0) | (a >= 2.0 ** -30) & (a <= 2.0 ** 30)).all()): b.append("a value of " + k)
    if not ((d["nx"] >= 0) & (d["nx"] < C)).all(): b.append("an entry of nx")
    else:
        e = np.concatenate([gentries(d["nx"][r]) for r in range(N)])
        at, back = np.zeros(8 * N, np.int64), np.zeros(8 * N, np.int64)
        for i in range(1, C + 1):
            at = e[np.arange(8 * N), at]
            back = np.where((at == 0) & (back == 0), i, back)
        if not (back == C).all(): b.append("a ring of nx")
    none, least, most = [emit(mx_ref.quantize(np.full((128, 16), k, np.float32).astype(BF)))[1][0, 0] for k in (0.0, 2.0 ** -8, 2.0 ** 8)]
    for r in range(N):
        if ((d["wc"][r] == 0x7F) | (d["wc"][r] == 0xFF)).any(): b.append("wc: a code that is no number")
        s = mx_ref.live(d["ws"][r])
        if ((s != none) & ((s < least) | (s > most))).any(): b.append("ws: a scale out of range")
    return b
def at(a, e):
    return np.take_along_axis(a, e, axis=1)
def mean(a, b):
    return ((a.astype(np.float32) + b.astype(np.float32)) * np.float32(0.5)).astype(BF)
def reference(x, u, v, nx, wc, ws):
    qu = [mx_ref.quantize(u[r]) for r in range(N)]
    lay = [pk(wc[r], ws[r]) for r in range(N)]
    ring = [gentries(nx[r]).astype(np.int64) for r in range(N)]
    now = [x[r] for r in range(N)]
    for m in MASK:
        t, new, back, z = [], [], [], []
        for r in range(N):
            q = mx_ref.quantize(now[r])
            t.append(decode(q).astype(BF))
            up = mx_ref.matmul(qu[r], q)[::16] > 0
            guest = ring[r ^ m]
            host = np.argsort(guest, axis=1)
            leave = up & ~at(up, host)
            a = ring[r]
            for i in range(8):
                a = np.where(at(leave, a), at(a, a), a)
            new.append(np.where(leave, at(a, host), np.where(at(leave, guest), guest, a)))
            back.append(np.argsort(new[r], axis=1))
            z.append(mx_ref.quantize(mean(gcols(t[r], new[r]), gcols(t[r], back[r]))))
        for r in range(N):
            h = tile([mx_ref.matmul(pick(lay[r], np.arange(128 * b, 128 * b + 128)), z[r ^ m]) * np.float32(0.03125) for b in range(4)])
            now[r] = mean(gcols(t[r], back[r]), gcols(h, new[r]))
        ring = new
    y, nr = np.zeros((N, 128, C), np.float32), np.zeros((N, 8, C), np.float32)
    oc, osc = np.zeros((N, 128, 4 * C), np.uint8), np.zeros((N, 16, C), np.uint8)
    for r in range(N):
        q = mx_ref.quantize(now[r])
        y[r] = mx_ref.matmul(mx_ref.quantize(v[r]), q)
        nr[r] = ring[r]
        oc[r], osc[r] = emit(q)
    return {"y": y, "nr": nr, "oc": oc, "osc": osc}

@@ -1,0 +1,466 @@
+from concourse.mybir import dt, AluOpType, AxisListType, ActivationFunctionType
+
+ADD, SUB, MUL, MAX = AluOpType.add, AluOpType.subtract, AluOpType.mult, AluOpType.max
+GT, EQ, NE = AluOpType.is_gt, AluOpType.is_equal, AluOpType.not_equal
+COPY, IDENT = ActivationFunctionType.Copy, ActivationFunctionType.Identity
+C = 416
+K = C // 16
+MASKS = [1, 2, 3]
+HALF = [(0, 224), (224, 416)]
+CHUNK = [(4, 0, 16, 16), (5, 0, 32, 32), (6, 0, 64, 64), (7, 0, 128, 128), (7, 128, 256, 256), (7, 256, 288, 384)]
+
+
+def layout(items):
+    at, n = {}, 0
+    for name, w in items:
+        at[name] = (n, w)
+        n += (w + 15) // 16 * 16
+    return at, n
+
+
+_rb = [(k, C) for k in ("mask", "hm", "iota", "t16", "i207", "rR0", "rm0", "rs0", "om", "os", "W0")]
+_rb += [("%s%d" % (k, s), C) for s in range(1, 8) for k in "WMS"] + [("M0", C), ("S0", C)]
+_rb += [("mb%d" % s, 16) for s in range(4)] + [("og%d" % s, 16) for s in range(4)]
+_rb += [("%s_%d" % (k, r), 432) for r in (1, 2, 3) for k in ("up", "sg", "g", "l", "lm", "ls", "so", "go", "PB", "pm", "ps", "OB", "am", "as", "rR", "hm", "hs")]
+RB, NRB = layout(_rb)
+_ru = [("G%d" % s, K) for s in range(1, 8)] + [("OG0", K), ("pick", 8)] + [("q%d" % s, 1) for s in range(5)]
+_ru += [("%s_%d" % (k, r), K) for r in (1, 2, 3) for k in ("x", "sc", "ai", "bi", "og")]
+RU, NRU = layout(_ru)
+_rf = [("cx", C), ("eq1", C), ("nr", C), ("p16", 1), ("p17", 1), ("half", 1), ("bit", 4), ("nbit", 4)]
+_rf += [("f%d" % s, 1) for s in range(5)] + [("red%d" % s, 1) for s in range(4)]
+_rf += [("%s_%d" % (k, r), C) for r in (1, 2, 3) for k in ("bf", "bs", "of", "os")]
+_rf += [("%s_%d" % (k, r), K) for r in (1, 2, 3) for k in ("t2", "t3", "rG", "dG")]
+RF, NRF = layout(_rf)
+RI, NRI = layout([("nx", K), ("p", 1), ("p16", 1), ("bit", 4), ("pick", 8)])
+WHERE = {"rb": RB, "ru": RU, "rf": RF, "ri": RI}
+
+X4, U8, BF = "float8_e4m3fn_x4", "uint8", "bfloat16"
+SCRATCH = {
+    "rb": ("sbuf", [128, NRB], BF), "ru": ("sbuf", [128, NRU], "uint16"), "rf": ("sbuf", [128, NRF], "float32"), "ri": ("sbuf", [128, NRI], "int32"),
+    "et": ("sbuf", [128, 528], BF), "qe": ("sbuf", [128, 512], X4), "se": ("sbuf", [128, 512], U8),
+    "uin": ("sbuf", [128, 512], BF), "qu": ("sbuf", [128, 128], X4), "su": ("sbuf", [128, 128], U8),
+    "u2": ("sbuf", [128, 128], X4), "s2": ("sbuf", [128, 128], U8),
+    "vin": ("sbuf", [128, 512], BF), "qv": ("sbuf", [128, 128], X4), "sv": ("sbuf", [128, 128], U8),
+    "wq": ("sbuf", [128, 512], X4), "wp": ("sbuf", [128, 512], U8),
+    "yo": ("sbuf", [128, C], "float32"),
+    "psA": ("psum", [128, 2048], "float32"), "psB": ("psum", [128, 2048], "float32"),
+    "L0": ("sbuf", [128, 2 * K], "uint16"),
+    "xt0": ("sbuf", [128, 4 * C], BF), "xq0": ("sbuf", [128, C], X4), "xs0": ("sbuf", [128, C], U8),
+}
+for _r in (1, 2, 3):
+    for _n in ("th", "tp", "za", "zt", "hh", "tb", "xt"):
+        SCRATCH["%s%d" % (_n, _r)] = ("sbuf", [128, 4 * C], BF)
+    for _n in ("xq", "lq", "zq"):
+        SCRATCH["%s%d" % (_n, _r)] = ("sbuf", [128, C], X4)
+    for _n in ("xs", "lp", "zs"):
+        SCRATCH["%s%d" % (_n, _r)] = ("sbuf", [128, C], U8)
+    for _n in ("L", "LN", "LZ"):
+        SCRATCH["%s%d" % (_n, _r)] = ("sbuf", [128, 2 * K], "uint16")
+SEMAPHORES = ["cv", "cs", "ct", "cg", "dnx", "dx", "du", "dv", "dwc", "dws", "dout", "lsem"] + ["%s%d" % (k, r) for r in (1, 2, 3) for k in ("aN", "aZ", "aQ")]
+
+
+def rank_program(g, core, T, topo):
+    rank = T.rank_of(core)
+    if rank is None:
+        return
+    eng = {"v": g.vector, "s": g.scalar, "t": g.tensor, "g": g, "y": g.sync}
+    known = {q: {} for q in eng}
+    count = {q: 0 for q in eng}
+    clocks, wr, rd, total = {}, {}, {}, {}
+
+    def over(a, b):
+        return a[1] < b[2] and b[1] < a[2]
+
+    def learn(q, sem, n):
+        for k, v in list(clocks.get((sem, n), {}).items()) + [(sem, n)]:
+            if known[q].get(k, 0) < v:
+                known[q][k] = v
+
+    def sync(q, reads, writes):
+        need = {}
+        for r in reads:
+            for reg, ev in wr.get(r[0], []):
+                if over(reg, r):
+                    need[ev] = 1
+            if r[0][:2] == "ps":
+                for reg, ev in rd.get(r[0], []):
+                    if over(reg, r) and ev[0] != "c" + q:
+                        need[ev] = 1
+        for w in writes:
+            for reg, ev in wr.get(w[0], []) + rd.get(w[0], []):
+                if over(reg, w):
+                    need[ev] = 1
+        for sem, n in sorted(need, key=lambda e: -len(clocks.get(e, {})) * 100000 - e[1]):
+            if known[q].get(sem, 0) < n:
+                eng[q].wait_ge(T.sem[sem], n)
+                learn(q, sem, n)
+
+    def mark(ev, q, reads, writes):
+        clocks[ev] = dict(known[q]) if q else {}
+        for w in writes:
+            wr[w[0]] = [e for e in wr.get(w[0], []) if not (w[1] <= e[0][1] and e[0][2] <= w[2])] + [(w, ev)]
+            rd[w[0]] = [e for e in rd.get(w[0], []) if not (w[1] <= e[0][1] and e[0][2] <= w[2])]
+        for r in reads:
+            rd.setdefault(r[0], []).append((r, ev))
+
+    def op(q, f, reads, writes):
+        sync(q, reads, writes)
+        count[q] += 1
+        sem = "c" + q
+        f().then_inc(T.sem[sem], 1)
+        total[sem] = count[q]
+        mark((sem, count[q]), q, reads, writes)
+
+    def dma(q, sem, out, in_, reads, writes):
+        sync(q, reads, writes)
+        eng[q].dma_start(out, in_).then_inc(T.sem[sem], 16)
+        total[sem] = total.get(sem, 0) + 16
+        mark((sem, total[sem]), q, reads, writes)
+
+    def A(buf, a, b, step=1):
+        return (T[buf][:, a:b] if step == 1 else T[buf][:, a:b:step], [(buf, a, b)])
+
+    def N(buf, name, a=0, b=None):
+        o, w = WHERE[buf][name]
+        return A(buf, o + a, o + (w if b is None else b))
+
+    def ends(buf, name, n=C):
+        o = WHERE[buf][name][0]
+        return A(buf, o + 15, o + n, 16)
+
+    def ind(w, o):
+        return (w[0].indirect(o[0]), w[1] + o[1])
+
+    def P(buf, bank, n):
+        return (T[buf][:, 512 * bank:512 * bank + n], [(buf, 512 * bank, 512 * bank + 512)])
+
+    def plane(buf, b, a=0, e=C):
+        return A(buf, C * b + a, C * b + e)
+
+    def strip(buf, b, a, e):
+        return (T[buf][:, 4 * a + b:4 * e:4], [("%s#%d" % (buf, b), a, e)])
+
+    def tt(out, a, b, o):
+        op("v", lambda: g.vector.tensor_tensor(out[0], a[0], b[0], o), a[1] + b[1], out[1])
+
+    def ts(out, a, s1, o1, s2=None, o2=None):
+        regs = list(a[1])
+        if isinstance(s1, tuple):
+            regs += s1[1]
+            s1 = s1[0]
+        if isinstance(s2, tuple):
+            regs += s2[1]
+            s2 = s2[0]
+        if o2 is None:
+            op("v", lambda: g.vector.tensor_scalar(out[0], a[0], s1, None, o1), regs, out[1])
+        else:
+            op("v", lambda: g.vector.tensor_scalar(out[0], a[0], s1, s2, o1, o2), regs, out[1])
+
+    def vcopy(out, a):
+        op("v", lambda: g.vector.tensor_copy(out[0], a[0]), a[1], out[1])
+
+    def act(out, a, scale=1.0, bias=0.0):
+        if bias == 0.0 and scale == 1.0:
+            op("s", lambda: g.scalar.activation(out[0], a[0], COPY), a[1], out[1])
+        else:
+            op("s", lambda: g.scalar.activation(out[0], a[0], IDENT, bias=bias, scale=scale), a[1], out[1])
+
+    def scan(out, a, b, init, o1, o2):
+        op("v", lambda: g.vector.tensor_tensor_scan(out[0], a[0], b[0], init, o1, o2), a[1] + b[1], out[1])
+
+    def memset(out, v):
+        op("v", lambda: g.vector.memset(out[0], v), [], out[1])
+
+    def iota(out, pattern, base, cm):
+        op("g", lambda: g.iota(out[0], pattern, base, cm, allow_small_or_imprecise_dtypes=True), [], out[1])
+
+    def quant(q, s, tile, a, e, t0=None):
+        regs = [("%s#%d" % (tile, b), a, e) for b in range(4)] if t0 is None else [(tile, t0, t0 + 4 * (e - a))]
+        i0 = 4 * a if t0 is None else t0
+        op("v", lambda: g.vector.quantize_mx(T[q][:, a:e], T[s][:, a:e], T[tile][:, i0:i0 + 4 * (e - a)]), regs, [(q, a, e), (s, a, e)])
+
+    def mm(out, lq, ls, la, rq, rs, a, e):
+        op("t", lambda: g.tensor.matmul_mx(out[0], T[lq][:, la:la + 128], T[ls][:, la:la + 128], T[rq][:, a:e], T[rs][:, a:e], True, True),
+           [(lq, la, la + 128), (ls, la, la + 128), (rq, a, e), (rs, a, e)], out[1])
+
+    def peer(m):
+        return T.cores[rank ^ m]
+
+    def send(dst, sem, pairs, regs):
+        rid, pid = topo.addr(dst)[:2]
+        mask = topo.mask(core, dst)
+        n = len(topo.engines(core, dst))
+        sync("g", regs, [])
+        for out, in_ in pairs:
+            g.remote_dma(out, in_, T.sem[sem], T.sem.lsem, pid, rid, mask)
+            total["lsem"] = total.get("lsem", 0) + n
+
+    def arrives(src, sem, k, regs):
+        n = k * len(topo.engines(src, core))
+        total[sem] = n
+        mark((sem, n), None, [], regs)
+
+    def send_lists(src, dst_buf, sem, m):
+        send(peer(m), sem, [(T[dst_buf][:, 0:2 * K], T[src][:, 0:2 * K])], [(src, 0, 2 * K)])
+        arrives(peer(m), sem, 1, [(dst_buf, 0, 2 * K)])
+
+    def send_state(r, m):
+        xq, xs, lq, lp = "xq%d" % (r - 1), "xs%d" % (r - 1), "lq%d" % r, "lp%d" % r
+        send(peer(m), "aQ%d" % r, [(T[lq][:, 0:C].bitcast(dt.uint8), T[xq][:, 0:C].bitcast(dt.uint8)), (T[lp][:, 0:C], T[xs][:, 0:C])], [(xq, 0, C), (xs, 0, C)])
+        arrives(peer(m), "aQ%d" % r, 2, [(lq, 0, C), (lp, 0, C)])
+
+    def scores(r):
+        for i, (a, e) in enumerate(HALF):
+            mm(P("psB", i, e - a), "u2", "s2", 0, "xq%d" % (r - 1), "xs%d" % (r - 1), a, e)
+
+    def unpack(ps, q, s):
+        for b in range(4):
+            mm(P(ps, b, C), "qe", "se", 128 * b, q, s, 0, C)
+
+    def halves(ps, dst):
+        for b in range(4):
+            act(plane(dst, b), P(ps, b, C), scale=0.5)
+
+    mask, hm, io = N("rb", "mask"), N("rb", "hm"), N("rb", "iota")
+
+    def settle(m, s, n=C):
+        scan(N("rb", s, 0, n), N("rb", "hm", 0, n), N("rb", m, 0, n), 0.0, MUL, ADD)
+
+    def settle_max(src, dst, out, shift):
+        scan(N("rf", dst), N("rf", "cx"), N("rf", src), 0.0, MUL, MAX)
+        ts(out, ends("rf", dst), N("rf", "half"), MUL, shift, ADD)
+
+    dma("y", "dnx", N("ri", "nx")[0], T.nx[:], [], N("ri", "nx")[1])
+    dma("s", "dx", T.xt0[:], T.x[:], [], [("xt0", 0, 4 * C)])
+    dma("y", "du", T.uin[:], T.u[:], [], [("uin", 0, 512)])
+    dma("y", "dwc", T.wq[:].bitcast(dt.uint8), T.wc[:], [], [("wq", 0, 512)])
+    dma("y", "dws", T.wp[:], T.ws[:], [], [("wp", 0, 512)])
+    dma("y", "dv", T.vin[:], T.v[:], [], [("vin", 0, 512)])
+
+    op("g", lambda: g.iota(N("ri", "p")[0], [[0, 1]], 0, 1), [], N("ri", "p")[1])
+    iota(N("rb", "t16"), [[0, K], [1, 16]], 0, 0)
+    iota(io, [[1, C]], -208, 0)
+    memset(A("et", 0, 528), 1.0)
+    memset(N("rf", "f0"), -208.0)
+    memset(N("ru", "q0"), 0)
+    ts(N("ri", "p16"), N("ri", "p"), 15, AluOpType.bitwise_and)
+    for s in range(4):
+        ts(N("ri", "bit", s, s + 1), N("ri", "p"), s, AluOpType.logical_shift_right, 1, AluOpType.bitwise_and)
+    vcopy(N("rf", "p16"), N("ri", "p16"))
+    vcopy(N("rf", "bit"), N("ri", "bit"))
+    ts(N("rf", "p17"), N("rf", "p16"), 1.0, ADD)
+    ts(N("rf", "nbit"), N("rf", "bit"), -1.0, MUL, 1.0, ADD)
+    ts(mask, N("rb", "t16"), N("rf", "p16"), EQ)
+    ts(hm, N("rb", "t16"), N("rf", "p16"), NE)
+    ts(N("rf", "eq1"), N("rb", "t16"), N("rf", "p17"), EQ)
+    for s in range(4):
+        ts(N("rb", "mb%d" % s), N("rb", "mask", 0, 16), N("rf", "bit", s, s + 1), MUL)
+    ts(N("rf", "half"), N("rb", "mask", 15, 16), 0.5, MUL, 0.5, ADD)
+    tt(N("rf", "cx"), N("rf", "eq1"), hm, ADD)
+    iota(N("rb", "i207"), [[1, C]], -207, 0)
+    op("g", lambda: g.iota(N("ri", "pick")[0], [[16, 8]], 0, 0), [], N("ri", "pick")[1])
+    op("g", lambda: g.affine_select(T.et[:, 0:515], T.et[:, 0:515], [[1, 515]], EQ, 0.0, -3, -4), [("et", 0, 515)], [("et", 0, 515)])
+
+    vcopy(A("L0", 0, K), N("ri", "nx"))
+    w0 = N("rb", "W0")
+    op("v", lambda: g.vector.tensor_copy(w0[0].indirect(T.L0[:, 0:K]), io[0]), io[1] + [("L0", 0, K)], w0[1])
+    tt(N("rb", "M0"), w0, mask, MUL)
+    settle("M0", "S0")
+    ts(A("L0", K, 2 * K), ends("rb", "S0"), 208.0, ADD)
+    send_lists("L0", "LN1", "aN1", MASKS[0])
+
+    def first_x():
+        quant("xq0", "xs0", "xt0", 0, C, 0)
+        send_state(1, MASKS[0])
+
+    def first_u():
+        quant("qu", "su", "uin", 0, 128, 0)
+        vcopy(N("ru", "pick"), N("ri", "pick"))
+        pk = N("ru", "pick")
+        op("v", lambda: g.vector.tensor_copy(T.u2[:, 0:128].bitcast(dt.uint32), T.qu[:, 0:128].bitcast(dt.uint32).indirect(pk[0])), [("qu", 0, 128)] + pk[1], [("u2", 0, 128)])
+        op("s", lambda: g.scalar.activation(T.s2[:, 0:128], T.su[:, 0:128].indirect(pk[0]), COPY), [("su", 0, 128)] + pk[1], [("s2", 0, 128)])
+
+    def first_e():
+        for b in range(4):
+            op("v", lambda b=b: g.vector.quantize_mx(T.qe[:, 128 * b:128 * b + 128], T.se[:, 128 * b:128 * b + 128], T.et[:, 3 - b:515 - b]), [("et", 0, 515)], [("qe", 128 * b, 128 * b + 128), ("se", 128 * b, 128 * b + 128)])
+
+    def ups(r):
+        for i, (a, e) in enumerate(HALF):
+            ts(N("rb", "up_%d" % r, a, e), P("psB", i, e - a), 0.0, GT)
+        for i, (a, e) in reversed(list(enumerate(HALF))):
+            out, ps = N("rb", "sg_%d" % r, a, e), P("psB", i, e - a)
+            op("s", lambda: g.scalar.activation(out[0], ps[0], ActivationFunctionType.Sign), ps[1], out[1])
+
+    def chunk(c, part):
+        s, a, e, to = CHUNK[c]
+        n = e - a
+        if part == 0:
+            tt(N("rb", "om", to, to + n), ind(N("rb", "W%d" % s), N("ru", "OG0", a // 16, e // 16) if c else N("ru", "q4")), N("rb", "mask", 0, n), MUL)
+        if part == 1:
+            scan(N("rb", "os", to, to + n), N("rb", "hm", 0, n), N("rb", "om", to, to + n), 0.0, MUL, ADD)
+        if part == 2:
+            o = RB["os"][0]
+            ts(N("ru", "OG0", to // 16, to // 16 + n // 16), A("rb", o + to + 15, o + to + n, 16), 208.0, ADD)
+
+    for s in range(8):
+        src = A("L0", K, 2 * K) if s == 0 else N("ru", "G%d" % s)
+        w = N("rb", "W%d" % s)
+        big, small = s < 7, s < 4
+        if big:
+            act(N("rb", "W%d" % (s + 1)), ind(w, src))
+            if s:
+                tt(N("rb", "M%d" % s), ind(w, src), mask, MUL)
+            else:
+                tt(N("rb", "om"), ind(w, src), mask, MUL)
+        if small:
+            tt(N("rb", "og%d" % s), ind(w, N("ru", "q%d" % s)), N("rb", "mb%d" % s), MUL)
+        else:
+            chunk(s - 4, 0)
+        if big:
+            if s:
+                settle("M%d" % s, "S%d" % s)
+            else:
+                settle("om", "os")
+        if small:
+            op("v", lambda s=s: g.vector.tensor_reduce(N("rf", "red%d" % s)[0], N("rb", "og%d" % s)[0], AxisListType.X, ADD), N("rb", "og%d" % s)[1], N("rf", "red%d" % s)[1])
+        else:
+            chunk(s - 4, 1)
+        if big:
+            ts(N("ru", "G%d" % (s + 1)), ends("rb", "S%d" % s if s else "os"), 208.0, ADD)
+        if small:
+            ts(N("rf", "f%d" % (s + 1)), N("rf", "f%d" % s), N("rf", "nbit", s, s + 1), MUL, N("rf", "red%d" % s), ADD)
+            ts(N("ru", "q%d" % (s + 1)), N("rf", "f%d" % (s + 1)), 208.0, ADD)
+            if s == 3:
+                vcopy(N("ru", "OG0", 0, 1), N("ru", "q4"))
+        else:
+            chunk(s - 4, 2)
+        if s == 1:
+            first_x()
+            first_u()
+            scores(1)
+        if s == 3:
+            first_e()
+            unpack("psA", "xq0", "xs0")
+        if s == 4:
+            ups(1)
+    for c in (4, 5):
+        for part in range(3):
+            chunk(c, part)
+    halves("psA", "th1")
+    rr = N("rb", "rR0")
+    og = N("ru", "OG0")
+    op("v", lambda: g.vector.tensor_copy(rr[0].indirect(og[0]), N("rb", "i207")[0]), N("rb", "i207")[1] + og[1], rr[1])
+    tt(N("rb", "rm0"), rr, mask, MUL)
+    settle("rm0", "rs0")
+    rG = ends("rb", "rs0")
+    order = og
+
+    def hosts(r, rr, rG):
+        tt(N("rb", "hm_%d" % r, 0, C), ind(rr, A("LN%d" % r, K, 2 * K)), mask, MUL)
+        settle("hm_%d" % r, "hs_%d" % r)
+        tt(N("rf", "dG_%d" % r), ends("rb", "hs_%d" % r), rG, SUB)
+
+    for r in (1, 2, 3):
+        m = MASKS[r - 1]
+        L, LN, LZ = "L%d" % r, "LN%d" % r, "LZ%d" % r
+        nb = lambda k, a=0, b=C: N("rb", "%s_%d" % (k, r), a, b)
+        nu = lambda k: N("ru", "%s_%d" % (k, r))
+        nf = lambda k: N("rf", "%s_%d" % (k, r))
+        if r > 1:
+            ups(r)
+        tt(nb("g"), ind(nb("sg"), A(LN, 0, K)), nb("up"), GT)
+        act(nb("go"), ind(nb("g"), order))
+        vcopy(nb("l"), ind(nb("g"), A(LN, K, 2 * K)))
+        if r == 1:
+            hosts(1, rr, rG)
+        tt(nb("lm"), ind(nb("g"), A(LN, K, 2 * K)), mask, MUL)
+        act(nb("so"), ind(nb("l"), order), scale=-1.0, bias=1.0)
+        settle("lm_%d" % r, "ls_%d" % r)
+        lG = ends("rb", "ls_%d" % r)
+        tt(nf("t2"), lG, nf("dG"), MUL)
+        scan(nb("PB"), nb("so"), nb("go"), -208.0, ADD, ADD)
+        tt(nf("t3"), nf("t2"), rG, ADD)
+        ts(nu("x"), nf("t3"), 207.0, ADD)
+        if r == 1:
+            unpack("psB", "lq1", "lp1")
+            halves("psB", "tp1")
+        else:
+            halves("psA", "th%d" % r)
+        tt(nb("pm"), ind(nb("PB"), nu("x")), mask, MUL)
+        settle("pm_%d" % r, "ps_%d" % r)
+        tt(nf("rG"), ends("rb", "ps_%d" % r), lG, SUB)
+        rG = nf("rG")
+        ts(nu("sc"), rG, 208.0, ADD)
+        ts(nu("ai"), rG, 207.0, ADD)
+        ts(nu("bi"), rG, 209.0, ADD)
+        ob = nb("OB", 0, 417)
+        op("v", lambda: g.vector.tensor_copy(ob[0].indirect(nu("sc")[0]), io[0]), io[1] + nu("sc")[1], ob[1])
+        vcopy(nb("OB", 0, 1), nb("OB", 416, 417))
+        act(nb("OB", 417, 418), nb("OB", 1, 2))
+        tt(nb("am"), ind(nb("OB"), nu("ai")), mask, MUL)
+        act(nf("bf"), ind(nb("OB", 0, 418), nu("bi")), bias=1232.0)
+        settle("am_%d" % r, "as_%d" % r)
+        ts(A(L, 0, K), ends("rb", "as_%d" % r), 208.0, ADD)
+        settle_max("bf_%d" % r, "bs_%d" % r, A(L, K, 2 * K), -1024.0)
+        send_lists(L, LZ, "aZ%d" % r, m)
+        if r < 3:
+            send_lists(L, "LN%d" % (r + 1), "aN%d" % (r + 1), MASKS[r])
+            act(nf("of"), nb("OB", 1, 417), bias=1232.0)
+            rr = nb("rR")
+            tt(rr, ind(nb("PB"), nu("x")), nb("l"), SUB)
+            settle_max("of_%d" % r, "os_%d" % r, nu("og"), -1024.0)
+            order = nu("og")
+        if r == 1:
+            quant("qv", "sv", "vin", 0, 128, 0)
+        else:
+            unpack("psB", "lq%d" % r, "lp%d" % r)
+            halves("psB", "tp%d" % r)
+        th, tp, tb, za, zt, hh, xt = ["%s%d" % (k, r) for k in ("th", "tp", "tb", "za", "zt", "hh", "xt")]
+        zq, zs, xq, xs = ["%s%d" % (k, r) for k in ("zq", "zs", "xq", "xs")]
+
+        def own(b):
+            act(plane(tb, b), ind(plane(th, b), A(L, K, 2 * K)))
+
+        own(0)
+        own(1)
+        for i, (a, e) in enumerate(HALF):
+            for b in range(4):
+                act(plane(za, b, a, e), ind(plane(tp, b), A(LZ, a // 16, e // 16)))
+                tt(strip(zt, b, a, e), ind(plane(tp, b), A(LZ, K + a // 16, K + e // 16)), plane(za, b, a, e), ADD)
+            quant(zq, zs, zt, a, e)
+            for b in range(4):
+                mm(P("psB" if i else "psA", b, e - a), "wq", "wp", 128 * b, zq, zs, a, e)
+        own(2)
+        own(3)
+        if r < 3:
+            hosts(r + 1, rr, rG)
+        else:
+            act(N("rf", "nr"), ind(nb("OB"), nu("ai")), bias=208.0)
+            dma("y", "dout", T.nr[:, :], T.rf[0:128:16, RF["nr"][0]:RF["nr"][0] + C], N("rf", "nr")[1], [])
+        for b in range(4):
+            a, e = HALF[0]
+            ts(plane(hh, b, a, e), P("psA", b, e - a), 0.015625, MUL)
+        for b in range(4):
+            a, e = HALF[1]
+            if b < 3:
+                act(plane(hh, b, a, e), P("psB", b, e - a), scale=0.015625)
+            else:
+                ts(plane(hh, b, a, e), P("psB", b, e - a), 0.015625, MUL)
+        for i, (a, e) in enumerate(HALF):
+            for b in range(4):
+                tt(strip(xt, b, a, e), ind(plane(hh, b), A(L, a // 16, e // 16)), plane(tb, b, a, e), ADD)
+            quant(xq, xs, xt, a, e)
+            if r == 3:
+                dma("y", "dout", T.oc[:, 4 * a:4 * e], T[xq][:, a:e].bitcast(dt.uint8), [(xq, a, e)], [])
+                for k in range(4):
+                    dma("y", "dout", T.osc[4 * k:4 * k + 4, a:e], T[xs][32 * k:32 * k + 4, a:e], [(xs, a, e)], [])
+                mm(P("psA", i, e - a), "qv", "sv", 0, xq, xs, a, e)
+                act(A("yo", a, e), P("psA", i, e - a))
+                dma("s", "dout", T.y[:, a:e], T.yo[:, a:e], [("yo", a, e)], [])
+        if r < 3:
+            send_state(r + 1, MASKS[r])
+            scores(r + 1)
+            unpack("psA", xq, xs)
+
+    for sem in sorted(total):
+        g.wait_ge(T.sem[sem], total[sem])

@@ -6,7 +6,7 @@ COPY, IDENT = ActivationFunctionType.Copy, ActivationFunctionType.Identity
 C = 416
 K = C // 16
 MASKS = [1, 2, 3]
-HALF = [(0, 224), (224, 416)]
+HALF = [(0, 256), (256, 416)]
 CHUNK = [(4, 0, 16, 16), (5, 0, 32, 32), (6, 0, 64, 64), (7, 0, 128, 128), (7, 128, 256, 256), (7, 256, 288, 384)]
 
 
@@ -18,18 +18,18 @@ def layout(items):
     return at, n
 
 
-_rb = [(k, C) for k in ("mask", "hm", "iota", "t16", "i207", "rR0", "rm0", "rs0", "om", "os", "W0")]
-_rb += [("%s%d" % (k, s), C) for s in range(1, 8) for k in "WMS"] + [("M0", C), ("S0", C)]
-_rb += [("mb%d" % s, 16) for s in range(4)] + [("og%d" % s, 16) for s in range(4)]
-_rb += [("%s_%d" % (k, r), 432) for r in (1, 2, 3) for k in ("up", "sg", "g", "l", "lm", "ls", "so", "go", "PB", "pm", "ps", "OB", "am", "as", "rR", "hm", "hs")]
+_rb = [(k, C) for k in ("mask", "hm", "cx", "one", "two", "iota", "t16", "om", "os", "W0")]
+_rb += [("%s%d" % (k, s), C) for s in range(1, 8) for k in "WMS"]
+_rb += [("mb%d" % s, 16) for s in range(4)] + [("og%d" % s, 16) for s in range(4)] + [("ds%d" % s, 16) for s in range(4)] + [("cp", 16)]
+_rb += [("%s_%d" % (k, r), 432) for r in (1, 2, 3) for k in ("up", "sg", "g", "l", "ls", "so", "go", "PB", "pm", "ps", "OB", "am", "as", "rR", "hm", "hs")]
 RB, NRB = layout(_rb)
 _ru = [("G%d" % s, K) for s in range(1, 8)] + [("OG0", K), ("pick", 8)] + [("q%d" % s, 1) for s in range(5)]
 _ru += [("%s_%d" % (k, r), K) for r in (1, 2, 3) for k in ("x", "sc", "ai", "bi", "og")]
 RU, NRU = layout(_ru)
-_rf = [("cx", C), ("eq1", C), ("nr", C), ("p16", 1), ("p17", 1), ("half", 1), ("bit", 4), ("nbit", 4)]
-_rf += [("f%d" % s, 1) for s in range(5)] + [("red%d" % s, 1) for s in range(4)]
+_rf = [(k, C) for k in ("i1024", "w0", "w0s", "rr", "rrs", "hf", "hfs", "nr")]
+_rf += [("p16", 1), ("pw", 16), ("bit", 4), ("f0", 1), ("rG0", K), ("hd", K)] + [("fo%d" % s, 16) for s in range(4)]
 _rf += [("%s_%d" % (k, r), C) for r in (1, 2, 3) for k in ("bf", "bs", "of", "os")]
-_rf += [("%s_%d" % (k, r), K) for r in (1, 2, 3) for k in ("t2", "t3", "rG", "dG")]
+_rf += [("%s_%d" % (k, r), K) for r in (1, 2, 3) for k in ("t2", "t3", "lG", "rG", "rH", "dG")]
 RF, NRF = layout(_rf)
 RI, NRI = layout([("nx", K), ("p", 1), ("p16", 1), ("bit", 4), ("pick", 8)])
 WHERE = {"rb": RB, "ru": RU, "rf": RF, "ri": RI}
@@ -166,7 +166,11 @@ def rank_program(g, core, T, topo):
             op("s", lambda: g.scalar.activation(out[0], a[0], IDENT, bias=bias, scale=scale), a[1], out[1])
 
     def scan(out, a, b, init, o1, o2):
-        op("v", lambda: g.vector.tensor_tensor_scan(out[0], a[0], b[0], init, o1, o2), a[1] + b[1], out[1])
+        regs = a[1] + b[1]
+        if isinstance(init, tuple):
+            regs = regs + init[1]
+            init = init[0]
+        op("v", lambda: g.vector.tensor_tensor_scan(out[0], a[0], b[0], init, o1, o2), regs, out[1])
 
     def memset(out, v):
         op("v", lambda: g.vector.memset(out[0], v), [], out[1])
@@ -226,9 +230,9 @@ def rank_program(g, core, T, topo):
     def settle(m, s, n=C):
         scan(N("rb", s, 0, n), N("rb", "hm", 0, n), N("rb", m, 0, n), 0.0, MUL, ADD)
 
-    def settle_max(src, dst, out, shift):
-        scan(N("rf", dst), N("rf", "cx"), N("rf", src), 0.0, MUL, MAX)
-        ts(out, ends("rf", dst), N("rf", "half"), MUL, shift, ADD)
+    def settle_max(buf, src, dst, out, shift):
+        scan(N(buf, dst, 0, C), N("rb", "cx"), N(buf, src, 0, C), 0.0, MUL, MAX)
+        ts(out, ends(buf, dst), N("rf", "pw", 15, 16), MUL, shift, ADD)
 
     dma("y", "dnx", N("ri", "nx")[0], T.nx[:], [], N("ri", "nx")[1])
     dma("s", "dx", T.xt0[:], T.x[:], [], [("xt0", 0, 4 * C)])
@@ -238,35 +242,39 @@ def rank_program(g, core, T, topo):
     dma("y", "dv", T.vin[:], T.v[:], [], [("vin", 0, 512)])
 
     op("g", lambda: g.iota(N("ri", "p")[0], [[0, 1]], 0, 1), [], N("ri", "p")[1])
+    memset(A("et", 0, 515), 1.0)
+    op("g", lambda: g.affine_select(T.et[:, 0:515], T.et[:, 0:515], [[1, 515]], EQ, 0.0, -3, -4), [("et", 0, 515)], [("et", 0, 515)])
     iota(N("rb", "t16"), [[0, K], [1, 16]], 0, 0)
-    iota(io, [[1, C]], -208, 0)
-    memset(A("et", 0, 528), 1.0)
+    op("g", lambda: g.iota(N("ri", "pick")[0], [[16, 8]], 0, 0), [], N("ri", "pick")[1])
+    memset(N("rb", "one"), 1.0)
     memset(N("rf", "f0"), -208.0)
     memset(N("ru", "q0"), 0)
+    scan(N("rf", "i1024"), N("rb", "one"), N("rb", "one"), 1023.0, MUL, ADD)
+    act(io, N("rf", "i1024"), bias=-1232.0)
+    act(N("rb", "two"), N("rb", "one"), scale=2.0)
     ts(N("ri", "p16"), N("ri", "p"), 15, AluOpType.bitwise_and)
     for s in range(4):
         ts(N("ri", "bit", s, s + 1), N("ri", "p"), s, AluOpType.logical_shift_right, 1, AluOpType.bitwise_and)
     vcopy(N("rf", "p16"), N("ri", "p16"))
     vcopy(N("rf", "bit"), N("ri", "bit"))
-    ts(N("rf", "p17"), N("rf", "p16"), 1.0, ADD)
-    ts(N("rf", "nbit"), N("rf", "bit"), -1.0, MUL, 1.0, ADD)
-    ts(mask, N("rb", "t16"), N("rf", "p16"), EQ)
-    ts(hm, N("rb", "t16"), N("rf", "p16"), NE)
-    ts(N("rf", "eq1"), N("rb", "t16"), N("rf", "p17"), EQ)
     for s in range(4):
-        ts(N("rb", "mb%d" % s), N("rb", "mask", 0, 16), N("rf", "bit", s, s + 1), MUL)
-    ts(N("rf", "half"), N("rb", "mask", 15, 16), 0.5, MUL, 0.5, ADD)
-    tt(N("rf", "cx"), N("rf", "eq1"), hm, ADD)
-    iota(N("rb", "i207"), [[1, C]], -207, 0)
-    op("g", lambda: g.iota(N("ri", "pick")[0], [[16, 8]], 0, 0), [], N("ri", "pick")[1])
-    op("g", lambda: g.affine_select(T.et[:, 0:515], T.et[:, 0:515], [[1, 515]], EQ, 0.0, -3, -4), [("et", 0, 515)], [("et", 0, 515)])
+        act(N("rb", "ds%d" % s), N("rb", "one", 0, 16))
+        ts(N("rb", "ds%d" % s, 0, 1), N("rf", "bit", s, s + 1), -1.0, MUL, 1.0, ADD)
+    for b in range(4):
+        op("v", lambda b=b: g.vector.quantize_mx(T.qe[:, 128 * b:128 * b + 128], T.se[:, 128 * b:128 * b + 128], T.et[:, 3 - b:515 - b]), [("et", 0, 515)], [("qe", 128 * b, 128 * b + 128), ("se", 128 * b, 128 * b + 128)])
 
     vcopy(A("L0", 0, K), N("ri", "nx"))
-    w0 = N("rb", "W0")
-    op("v", lambda: g.vector.tensor_copy(w0[0].indirect(T.L0[:, 0:K]), io[0]), io[1] + [("L0", 0, K)], w0[1])
-    tt(N("rb", "M0"), w0, mask, MUL)
-    settle("M0", "S0")
-    ts(A("L0", K, 2 * K), ends("rb", "S0"), 208.0, ADD)
+    w0 = N("rf", "w0")
+    op("v", lambda: g.vector.tensor_copy(w0[0].indirect(T.L0[:, 0:K]), N("rf", "i1024")[0]), N("rf", "i1024")[1] + [("L0", 0, K)], w0[1])
+    act(N("rb", "W0"), w0, bias=-1232.0)
+    ts(N("rb", "cx"), N("rb", "t16"), N("rf", "p16"), GT, 2.0, MUL)
+    ts(N("rb", "mask"), N("rb", "t16"), N("rf", "p16"), EQ)
+    ts(N("rb", "cp"), N("rb", "t16", 0, 16), N("rf", "p16"), GT, 0.5, MUL)
+    scan(N("rf", "pw"), N("rb", "cp"), N("rb", "mask", 0, 16), 0.0, MUL, ADD)
+    act(hm, N("rb", "mask"), scale=-1.0, bias=1.0)
+    settle_max("rf", "w0", "w0s", A("L0", K, 2 * K), -1024.0)
+    for s in range(4):
+        ts(N("rb", "mb%d" % s), N("rb", "mask", 0, 16), N("rf", "bit", s, s + 1), MUL)
     send_lists("L0", "LN1", "aN1", MASKS[0])
 
     def first_x():
@@ -279,10 +287,6 @@ def rank_program(g, core, T, topo):
         pk = N("ru", "pick")
         op("v", lambda: g.vector.tensor_copy(T.u2[:, 0:128].bitcast(dt.uint32), T.qu[:, 0:128].bitcast(dt.uint32).indirect(pk[0])), [("qu", 0, 128)] + pk[1], [("u2", 0, 128)])
         op("s", lambda: g.scalar.activation(T.s2[:, 0:128], T.su[:, 0:128].indirect(pk[0]), COPY), [("su", 0, 128)] + pk[1], [("s2", 0, 128)])
-
-    def first_e():
-        for b in range(4):
-            op("v", lambda b=b: g.vector.quantize_mx(T.qe[:, 128 * b:128 * b + 128], T.se[:, 128 * b:128 * b + 128], T.et[:, 3 - b:515 - b]), [("et", 0, 515)], [("qe", 128 * b, 128 * b + 128), ("se", 128 * b, 128 * b + 128)])
 
     def ups(r):
         for i, (a, e) in enumerate(HALF):
@@ -322,14 +326,13 @@ def rank_program(g, core, T, topo):
             else:
                 settle("om", "os")
         if small:
-            op("v", lambda s=s: g.vector.tensor_reduce(N("rf", "red%d" % s)[0], N("rb", "og%d" % s)[0], AxisListType.X, ADD), N("rb", "og%d" % s)[1], N("rf", "red%d" % s)[1])
+            scan(N("rf", "fo%d" % s), N("rb", "ds%d" % s), N("rb", "og%d" % s), N("rf", "fo%d" % (s - 1), 15, 16) if s else N("rf", "f0"), MUL, ADD)
         else:
             chunk(s - 4, 1)
         if big:
             ts(N("ru", "G%d" % (s + 1)), ends("rb", "S%d" % s if s else "os"), 208.0, ADD)
         if small:
-            ts(N("rf", "f%d" % (s + 1)), N("rf", "f%d" % s), N("rf", "nbit", s, s + 1), MUL, N("rf", "red%d" % s), ADD)
-            ts(N("ru", "q%d" % (s + 1)), N("rf", "f%d" % (s + 1)), 208.0, ADD)
+            ts(N("ru", "q%d" % (s + 1)), N("rf", "fo%d" % s, 15, 16), 208.0, ADD)
             if s == 3:
                 vcopy(N("ru", "OG0", 0, 1), N("ru", "q4"))
         else:
@@ -339,26 +342,19 @@ def rank_program(g, core, T, topo):
             first_u()
             scores(1)
         if s == 3:
-            first_e()
             unpack("psA", "xq0", "xs0")
         if s == 4:
             ups(1)
     for c in (4, 5):
         for part in range(3):
             chunk(c, part)
-    halves("psA", "th1")
-    rr = N("rb", "rR0")
-    og = N("ru", "OG0")
-    op("v", lambda: g.vector.tensor_copy(rr[0].indirect(og[0]), N("rb", "i207")[0]), N("rb", "i207")[1] + og[1], rr[1])
-    tt(N("rb", "rm0"), rr, mask, MUL)
-    settle("rm0", "rs0")
-    rG = ends("rb", "rs0")
-    order = og
+    rr = N("rf", "rr")
+    order = N("ru", "OG0")
+    op("v", lambda: g.vector.tensor_copy(rr[0].indirect(order[0]), N("rf", "i1024")[0]), N("rf", "i1024")[1] + order[1], rr[1])
+    act(N("rf", "hf"), ind(rr, A("LN1", K, 2 * K)))
+    rG = N("rf", "rG0")
+    settle_max("rf", "rr", "rrs", rG, -1231.0)
 
-    def hosts(r, rr, rG):
-        tt(N("rb", "hm_%d" % r, 0, C), ind(rr, A("LN%d" % r, K, 2 * K)), mask, MUL)
-        settle("hm_%d" % r, "hs_%d" % r)
-        tt(N("rf", "dG_%d" % r), ends("rb", "hs_%d" % r), rG, SUB)
 
     for r in (1, 2, 3):
         m = MASKS[r - 1]
@@ -370,22 +366,21 @@ def rank_program(g, core, T, topo):
             ups(r)
         tt(nb("g"), ind(nb("sg"), A(LN, 0, K)), nb("up"), GT)
         act(nb("go"), ind(nb("g"), order))
-        vcopy(nb("l"), ind(nb("g"), A(LN, K, 2 * K)))
+        tt(nb("l"), ind(nb("g"), A(LN, K, 2 * K)), N("rb", "two"), ADD)
+        act(nb("so"), ind(nb("l"), order), scale=-1.0, bias=3.0)
+        lG = nf("lG")
+        settle_max("rb", "l_%d" % r, "ls_%d" % r, lG, -2.0)
         if r == 1:
-            hosts(1, rr, rG)
-        tt(nb("lm"), ind(nb("g"), A(LN, K, 2 * K)), mask, MUL)
-        act(nb("so"), ind(nb("l"), order), scale=-1.0, bias=1.0)
-        settle("lm_%d" % r, "ls_%d" % r)
-        lG = ends("rb", "ls_%d" % r)
+            settle_max("rf", "hf", "hfs", N("rf", "hd"), -1231.0)
+            tt(nf("dG"), N("rf", "hd"), rG, SUB)
         tt(nf("t2"), lG, nf("dG"), MUL)
         scan(nb("PB"), nb("so"), nb("go"), -208.0, ADD, ADD)
         tt(nf("t3"), nf("t2"), rG, ADD)
         ts(nu("x"), nf("t3"), 207.0, ADD)
+        halves("psA", "th%d" % r)
         if r == 1:
             unpack("psB", "lq1", "lp1")
             halves("psB", "tp1")
-        else:
-            halves("psA", "th%d" % r)
         tt(nb("pm"), ind(nb("PB"), nu("x")), mask, MUL)
         settle("pm_%d" % r, "ps_%d" % r)
         tt(nf("rG"), ends("rb", "ps_%d" % r), lG, SUB)
@@ -401,14 +396,15 @@ def rank_program(g, core, T, topo):
         act(nf("bf"), ind(nb("OB", 0, 418), nu("bi")), bias=1232.0)
         settle("am_%d" % r, "as_%d" % r)
         ts(A(L, 0, K), ends("rb", "as_%d" % r), 208.0, ADD)
-        settle_max("bf_%d" % r, "bs_%d" % r, A(L, K, 2 * K), -1024.0)
+        settle_max("rf", "bf_%d" % r, "bs_%d" % r, A(L, K, 2 * K), -1024.0)
         send_lists(L, LZ, "aZ%d" % r, m)
         if r < 3:
             send_lists(L, "LN%d" % (r + 1), "aN%d" % (r + 1), MASKS[r])
             act(nf("of"), nb("OB", 1, 417), bias=1232.0)
             rr = nb("rR")
-            tt(rr, ind(nb("PB"), nu("x")), nb("l"), SUB)
-            settle_max("of_%d" % r, "os_%d" % r, nu("og"), -1024.0)
+            tt(rr, ind(nb("PB"), nu("x")), nb("l", 0, C), SUB)
+            ts(nf("rH"), rG, -2.0, ADD)
+            settle_max("rf", "of_%d" % r, "os_%d" % r, nu("og"), -1024.0)
             order = nu("og")
         if r == 1:
             quant("qv", "sv", "vin", 0, 128, 0)
@@ -418,11 +414,11 @@ def rank_program(g, core, T, topo):
         th, tp, tb, za, zt, hh, xt = ["%s%d" % (k, r) for k in ("th", "tp", "tb", "za", "zt", "hh", "xt")]
         zq, zs, xq, xs = ["%s%d" % (k, r) for k in ("zq", "zs", "xq", "xs")]
 
-        def own(b):
-            act(plane(tb, b), ind(plane(th, b), A(L, K, 2 * K)))
-
-        own(0)
-        own(1)
+        for b in range(4):
+            if b in ((3,), (1, 2), (1, 2, 3))[r - 1]:
+                vcopy(plane(tb, b), ind(plane(th, b), A(L, K, 2 * K)))
+            elif (r, b) != (2, 3):
+                act(plane(tb, b), ind(plane(th, b), A(L, K, 2 * K)))
         for i, (a, e) in enumerate(HALF):
             for b in range(4):
                 act(plane(za, b, a, e), ind(plane(tp, b), A(LZ, a // 16, e // 16)))
@@ -430,22 +426,22 @@ def rank_program(g, core, T, topo):
             quant(zq, zs, zt, a, e)
             for b in range(4):
                 mm(P("psB" if i else "psA", b, e - a), "wq", "wp", 128 * b, zq, zs, a, e)
-        own(2)
-        own(3)
         if r < 3:
-            hosts(r + 1, rr, rG)
-        else:
-            act(N("rf", "nr"), ind(nb("OB"), nu("ai")), bias=208.0)
-            dma("y", "dout", T.nr[:, :], T.rf[0:128:16, RF["nr"][0]:RF["nr"][0] + C], N("rf", "nr")[1], [])
+            tt(N("rb", "hm_%d" % (r + 1), 0, C), ind(rr, A("LN%d" % (r + 1), K, 2 * K)), mask, MUL)
+        a, e = HALF[0]
         for b in range(4):
-            a, e = HALF[0]
-            ts(plane(hh, b, a, e), P("psA", b, e - a), 0.015625, MUL)
+            act(plane(hh, b, a, e), P("psA", b, e - a), scale=0.015625)
+        a, e = HALF[1]
         for b in range(4):
-            a, e = HALF[1]
-            if b < 3:
+            if b % 2:
                 act(plane(hh, b, a, e), P("psB", b, e - a), scale=0.015625)
             else:
                 ts(plane(hh, b, a, e), P("psB", b, e - a), 0.015625, MUL)
+        if r == 2:
+            act(plane(tb, 3), ind(plane(th, 3), A(L, K, 2 * K)))
+        if r == 3:
+            act(N("rf", "nr"), ind(nb("OB"), nu("ai")), bias=208.0)
+            dma("y", "dout", T.nr[:, :], T.rf[0:128:16, RF["nr"][0]:RF["nr"][0] + C], N("rf", "nr")[1], [])
         for i, (a, e) in enumerate(HALF):
             for b in range(4):
                 tt(strip(xt, b, a, e), ind(plane(hh, b), A(L, a // 16, e // 16)), plane(tb, b, a, e), ADD)
@@ -461,6 +457,8 @@ def rank_program(g, core, T, topo):
             send_state(r + 1, MASKS[r])
             scores(r + 1)
             unpack("psA", xq, xs)
+            settle("hm_%d" % (r + 1), "hs_%d" % (r + 1))
+            tt(N("rf", "dG_%d" % (r + 1)), ends("rb", "hs_%d" % (r + 1)), nf("rH"), SUB)
 
     for sem in sorted(total):
         g.wait_ge(T.sem[sem], total[sem])

@@ -6,7 +6,7 @@ COPY, IDENT = ActivationFunctionType.Copy, ActivationFunctionType.Identity
 C = 416
 K = C // 16
 MASKS = [1, 2, 3]
-HALF = [(0, 256), (256, 416)]
+HALF = [(0, 288), (288, 416)]
 CHUNK = [(4, 0, 16, 16), (5, 0, 32, 32), (6, 0, 64, 64), (7, 0, 128, 128), (7, 128, 256, 256), (7, 256, 288, 384)]
 
 
@@ -215,7 +215,8 @@ def rank_program(g, core, T, topo):
 
     def scores(r):
         for i, (a, e) in enumerate(HALF):
-            mm(P("psB", i, e - a), "u2", "s2", 0, "xq%d" % (r - 1), "xs%d" % (r - 1), a, e)
+            for k in (0, 2):
+                mm(P("psB", i + k, e - a), "u2", "s2", 0, "xq%d" % (r - 1), "xs%d" % (r - 1), a, e)
 
     def unpack(ps, q, s):
         for b in range(4):
@@ -230,9 +231,14 @@ def rank_program(g, core, T, topo):
     def settle(m, s, n=C):
         scan(N("rb", s, 0, n), N("rb", "hm", 0, n), N("rb", m, 0, n), 0.0, MUL, ADD)
 
-    def settle_max(buf, src, dst, out, shift):
+    def settle_max(*jobs):
+        for buf, src, dst, out, shift in jobs:
+            hold(buf, src, dst)
+        for buf, src, dst, out, shift in jobs:
+            ts(out, ends(buf, dst), N("rf", "pw", 15, 16), MUL, shift, ADD)
+
+    def hold(buf, src, dst):
         scan(N(buf, dst, 0, C), N("rb", "cx"), N(buf, src, 0, C), 0.0, MUL, MAX)
-        ts(out, ends(buf, dst), N("rf", "pw", 15, 16), MUL, shift, ADD)
 
     dma("y", "dnx", N("ri", "nx")[0], T.nx[:], [], N("ri", "nx")[1])
     dma("s", "dx", T.xt0[:], T.x[:], [], [("xt0", 0, 4 * C)])
@@ -242,8 +248,6 @@ def rank_program(g, core, T, topo):
     dma("y", "dv", T.vin[:], T.v[:], [], [("vin", 0, 512)])
 
     op("g", lambda: g.iota(N("ri", "p")[0], [[0, 1]], 0, 1), [], N("ri", "p")[1])
-    memset(A("et", 0, 515), 1.0)
-    op("g", lambda: g.affine_select(T.et[:, 0:515], T.et[:, 0:515], [[1, 515]], EQ, 0.0, -3, -4), [("et", 0, 515)], [("et", 0, 515)])
     iota(N("rb", "t16"), [[0, K], [1, 16]], 0, 0)
     op("g", lambda: g.iota(N("ri", "pick")[0], [[16, 8]], 0, 0), [], N("ri", "pick")[1])
     memset(N("rb", "one"), 1.0)
@@ -257,24 +261,27 @@ def rank_program(g, core, T, topo):
         ts(N("ri", "bit", s, s + 1), N("ri", "p"), s, AluOpType.logical_shift_right, 1, AluOpType.bitwise_and)
     vcopy(N("rf", "p16"), N("ri", "p16"))
     vcopy(N("rf", "bit"), N("ri", "bit"))
+    vcopy(N("ru", "pick"), N("ri", "pick"))
+    ts(N("rb", "mask"), N("rb", "t16"), N("rf", "p16"), EQ)
+    ts(N("rb", "cp"), N("rb", "t16", 0, 16), N("rf", "p16"), GT, 0.5, MUL)
+    act(hm, N("rb", "mask"), scale=-1.0, bias=1.0)
+    ts(N("rb", "cx"), N("rb", "t16"), N("rf", "p16"), GT, 2.0, MUL)
+    scan(N("rf", "pw"), N("rb", "cp"), N("rb", "mask", 0, 16), 0.0, MUL, ADD)
     for s in range(4):
         act(N("rb", "ds%d" % s), N("rb", "one", 0, 16))
-        ts(N("rb", "ds%d" % s, 0, 1), N("rf", "bit", s, s + 1), -1.0, MUL, 1.0, ADD)
-    for b in range(4):
-        op("v", lambda b=b: g.vector.quantize_mx(T.qe[:, 128 * b:128 * b + 128], T.se[:, 128 * b:128 * b + 128], T.et[:, 3 - b:515 - b]), [("et", 0, 515)], [("qe", 128 * b, 128 * b + 128), ("se", 128 * b, 128 * b + 128)])
 
     vcopy(A("L0", 0, K), N("ri", "nx"))
     w0 = N("rf", "w0")
     op("v", lambda: g.vector.tensor_copy(w0[0].indirect(T.L0[:, 0:K]), N("rf", "i1024")[0]), N("rf", "i1024")[1] + [("L0", 0, K)], w0[1])
     act(N("rb", "W0"), w0, bias=-1232.0)
-    ts(N("rb", "cx"), N("rb", "t16"), N("rf", "p16"), GT, 2.0, MUL)
-    ts(N("rb", "mask"), N("rb", "t16"), N("rf", "p16"), EQ)
-    ts(N("rb", "cp"), N("rb", "t16", 0, 16), N("rf", "p16"), GT, 0.5, MUL)
-    scan(N("rf", "pw"), N("rb", "cp"), N("rb", "mask", 0, 16), 0.0, MUL, ADD)
-    act(hm, N("rb", "mask"), scale=-1.0, bias=1.0)
-    settle_max("rf", "w0", "w0s", A("L0", K, 2 * K), -1024.0)
+    hold("rf", "w0", "w0s")
     for s in range(4):
         ts(N("rb", "mb%d" % s), N("rb", "mask", 0, 16), N("rf", "bit", s, s + 1), MUL)
+    ts(A("L0", K, 2 * K), ends("rf", "w0s"), N("rf", "pw", 15, 16), MUL, -1024.0, ADD)
+    for s in range(4):
+        ts(N("rb", "ds%d" % s, 0, 1), N("rf", "bit", s, s + 1), -1.0, MUL, 1.0, ADD)
+    memset(A("et", 0, 515), 1.0)
+    op("g", lambda: g.affine_select(T.et[:, 0:515], T.et[:, 0:515], [[1, 515]], EQ, 0.0, -3, -4), [("et", 0, 515)], [("et", 0, 515)])
     send_lists("L0", "LN1", "aN1", MASKS[0])
 
     def first_x():
@@ -283,17 +290,18 @@ def rank_program(g, core, T, topo):
 
     def first_u():
         quant("qu", "su", "uin", 0, 128, 0)
-        vcopy(N("ru", "pick"), N("ri", "pick"))
         pk = N("ru", "pick")
         op("v", lambda: g.vector.tensor_copy(T.u2[:, 0:128].bitcast(dt.uint32), T.qu[:, 0:128].bitcast(dt.uint32).indirect(pk[0])), [("qu", 0, 128)] + pk[1], [("u2", 0, 128)])
         op("s", lambda: g.scalar.activation(T.s2[:, 0:128], T.su[:, 0:128].indirect(pk[0]), COPY), [("su", 0, 128)] + pk[1], [("s2", 0, 128)])
 
-    def ups(r):
-        for i, (a, e) in enumerate(HALF):
-            ts(N("rb", "up_%d" % r, a, e), P("psB", i, e - a), 0.0, GT)
-        for i, (a, e) in reversed(list(enumerate(HALF))):
-            out, ps = N("rb", "sg_%d" % r, a, e), P("psB", i, e - a)
-            op("s", lambda: g.scalar.activation(out[0], ps[0], ActivationFunctionType.Sign), ps[1], out[1])
+    def constant(b):
+        op("v", lambda: g.vector.quantize_mx(T.qe[:, 128 * b:128 * b + 128], T.se[:, 128 * b:128 * b + 128], T.et[:, 3 - b:515 - b]), [("et", 0, 515)], [("qe", 128 * b, 128 * b + 128), ("se", 128 * b, 128 * b + 128)])
+
+    def up(r, i):
+        a, e = HALF[i]
+        ts(N("rb", "up_%d" % r, a, e), P("psB", i + 2, e - a), 0.0, GT)
+        out, ps = N("rb", "sg_%d" % r, a, e), P("psB", i, e - a)
+        op("s", lambda: g.scalar.activation(out[0], ps[0], ActivationFunctionType.Sign), ps[1], out[1])
 
     def chunk(c, part):
         s, a, e, to = CHUNK[c]
@@ -306,54 +314,55 @@ def rank_program(g, core, T, topo):
             o = RB["os"][0]
             ts(N("ru", "OG0", to // 16, to // 16 + n // 16), A("rb", o + to + 15, o + to + n, 16), 208.0, ADD)
 
-    for s in range(8):
+    for s in range(5):
         src = A("L0", K, 2 * K) if s == 0 else N("ru", "G%d" % s)
         w = N("rb", "W%d" % s)
-        big, small = s < 7, s < 4
-        if big:
-            act(N("rb", "W%d" % (s + 1)), ind(w, src))
-            if s:
-                tt(N("rb", "M%d" % s), ind(w, src), mask, MUL)
-            else:
-                tt(N("rb", "om"), ind(w, src), mask, MUL)
+        small = s < 4
+        act(N("rb", "W%d" % (s + 1)), ind(w, src))
+        tt(N("rb", "M%d" % s if s else "om"), ind(w, src), mask, MUL)
         if small:
             tt(N("rb", "og%d" % s), ind(w, N("ru", "q%d" % s)), N("rb", "mb%d" % s), MUL)
         else:
             chunk(s - 4, 0)
-        if big:
-            if s:
-                settle("M%d" % s, "S%d" % s)
-            else:
-                settle("om", "os")
+        if s:
+            settle("M%d" % s, "S%d" % s)
+        else:
+            settle("om", "os")
         if small:
             scan(N("rf", "fo%d" % s), N("rb", "ds%d" % s), N("rb", "og%d" % s), N("rf", "fo%d" % (s - 1), 15, 16) if s else N("rf", "f0"), MUL, ADD)
         else:
             chunk(s - 4, 1)
-        if big:
-            ts(N("ru", "G%d" % (s + 1)), ends("rb", "S%d" % s if s else "os"), 208.0, ADD)
+        ts(N("ru", "G%d" % (s + 1)), ends("rb", "S%d" % s if s else "os"), 208.0, ADD)
         if small:
             ts(N("ru", "q%d" % (s + 1)), N("rf", "fo%d" % s, 15, 16), 208.0, ADD)
             if s == 3:
                 vcopy(N("ru", "OG0", 0, 1), N("ru", "q4"))
         else:
             chunk(s - 4, 2)
-        if s == 1:
-            first_x()
-            first_u()
-            scores(1)
-        if s == 3:
-            unpack("psA", "xq0", "xs0")
-        if s == 4:
-            ups(1)
-    for c in (4, 5):
+    act(N("rb", "W6"), ind(N("rb", "W5"), N("ru", "G5")))
+    act(N("rb", "M7"), ind(N("rb", "W6"), N("ru", "G5")))
+    act(N("rb", "W7"), ind(N("rb", "M7"), N("ru", "G5")))
+    for part in range(3):
+        chunk(1, part)
+    first_x()
+    for part in range(3):
+        chunk(2, part)
+    first_u()
+    scores(1)
+    for c in (3, 4, 5):
         for part in range(3):
             chunk(c, part)
+            if c < 5 and part < 2:
+                constant(2 * c - 6 + part)
+            if c == 5 and part < 2:
+                up(1, part)
+    unpack("psA", "xq0", "xs0")
     rr = N("rf", "rr")
     order = N("ru", "OG0")
     op("v", lambda: g.vector.tensor_copy(rr[0].indirect(order[0]), N("rf", "i1024")[0]), N("rf", "i1024")[1] + order[1], rr[1])
     act(N("rf", "hf"), ind(rr, A("LN1", K, 2 * K)))
     rG = N("rf", "rG0")
-    settle_max("rf", "rr", "rrs", rG, -1231.0)
+    hold("rf", "rr", "rrs")
 
 
     for r in (1, 2, 3):
@@ -363,20 +372,25 @@ def rank_program(g, core, T, topo):
         nu = lambda k: N("ru", "%s_%d" % (k, r))
         nf = lambda k: N("rf", "%s_%d" % (k, r))
         if r > 1:
-            ups(r)
+            up(r, 0)
+            up(r, 1)
         tt(nb("g"), ind(nb("sg"), A(LN, 0, K)), nb("up"), GT)
         act(nb("go"), ind(nb("g"), order))
+        if r == 1:
+            ts(rG, ends("rf", "rrs"), N("rf", "pw", 15, 16), MUL, -1231.0, ADD)
         tt(nb("l"), ind(nb("g"), A(LN, K, 2 * K)), N("rb", "two"), ADD)
         act(nb("so"), ind(nb("l"), order), scale=-1.0, bias=3.0)
         lG = nf("lG")
-        settle_max("rb", "l_%d" % r, "ls_%d" % r, lG, -2.0)
+        left = ("rb", "l_%d" % r, "ls_%d" % r, lG, -2.0)
         if r == 1:
-            settle_max("rf", "hf", "hfs", N("rf", "hd"), -1231.0)
+            settle_max(left, ("rf", "hf", "hfs", N("rf", "hd"), -1231.0))
             tt(nf("dG"), N("rf", "hd"), rG, SUB)
+        else:
+            settle_max(left)
         tt(nf("t2"), lG, nf("dG"), MUL)
-        scan(nb("PB"), nb("so"), nb("go"), -208.0, ADD, ADD)
         tt(nf("t3"), nf("t2"), rG, ADD)
         ts(nu("x"), nf("t3"), 207.0, ADD)
+        scan(nb("PB", 0, C), nb("so"), nb("go"), -208.0, ADD, ADD)
         halves("psA", "th%d" % r)
         if r == 1:
             unpack("psB", "lq1", "lp1")
@@ -395,8 +409,9 @@ def rank_program(g, core, T, topo):
         tt(nb("am"), ind(nb("OB"), nu("ai")), mask, MUL)
         act(nf("bf"), ind(nb("OB", 0, 418), nu("bi")), bias=1232.0)
         settle("am_%d" % r, "as_%d" % r)
+        hold("rf", "bf_%d" % r, "bs_%d" % r)
         ts(A(L, 0, K), ends("rb", "as_%d" % r), 208.0, ADD)
-        settle_max("rf", "bf_%d" % r, "bs_%d" % r, A(L, K, 2 * K), -1024.0)
+        ts(A(L, K, 2 * K), ends("rf", "bs_%d" % r), N("rf", "pw", 15, 16), MUL, -1024.0, ADD)
         send_lists(L, LZ, "aZ%d" % r, m)
         if r < 3:
             send_lists(L, "LN%d" % (r + 1), "aN%d" % (r + 1), MASKS[r])
@@ -404,7 +419,7 @@ def rank_program(g, core, T, topo):
             rr = nb("rR")
             tt(rr, ind(nb("PB"), nu("x")), nb("l", 0, C), SUB)
             ts(nf("rH"), rG, -2.0, ADD)
-            settle_max("rf", "of_%d" % r, "os_%d" % r, nu("og"), -1024.0)
+            settle_max(("rf", "of_%d" % r, "os_%d" % r, nu("og"), -1024.0))
             order = nu("og")
         if r == 1:
             quant("qv", "sv", "vin", 0, 128, 0)
@@ -419,13 +434,20 @@ def rank_program(g, core, T, topo):
                 vcopy(plane(tb, b), ind(plane(th, b), A(L, K, 2 * K)))
             elif (r, b) != (2, 3):
                 act(plane(tb, b), ind(plane(th, b), A(L, K, 2 * K)))
-        for i, (a, e) in enumerate(HALF):
-            for b in range(4):
-                act(plane(za, b, a, e), ind(plane(tp, b), A(LZ, a // 16, e // 16)))
-                tt(strip(zt, b, a, e), ind(plane(tp, b), A(LZ, K + a // 16, K + e // 16)), plane(za, b, a, e), ADD)
+        def pack_z(i):
+            a, e = HALF[i]
             quant(zq, zs, zt, a, e)
             for b in range(4):
                 mm(P("psB" if i else "psA", b, e - a), "wq", "wp", 128 * b, zq, zs, a, e)
+
+        for i, (a, e) in enumerate(HALF):
+            for b in range(4):
+                for a1, e1 in ((a, a + 96), (a + 96, e)) if (i, b) == (0, 0) else ((a, e),):
+                    act(plane(za, b, a1, e1), ind(plane(tp, b), A(LZ, a1 // 16, e1 // 16)))
+                    tt(strip(zt, b, a1, e1), ind(plane(tp, b), A(LZ, K + a1 // 16, K + e1 // 16)), plane(za, b, a1, e1), ADD)
+                if (i, b) == (1, 0):
+                    pack_z(0)
+        pack_z(1)
         if r < 3:
             tt(N("rb", "hm_%d" % (r + 1), 0, C), ind(rr, A("LN%d" % (r + 1), K, 2 * K)), mask, MUL)
         a, e = HALF[0]
@@ -442,22 +464,32 @@ def rank_program(g, core, T, topo):
         if r == 3:
             act(N("rf", "nr"), ind(nb("OB"), nu("ai")), bias=208.0)
             dma("y", "dout", T.nr[:, :], T.rf[0:128:16, RF["nr"][0]:RF["nr"][0] + C], N("rf", "nr")[1], [])
+        def pack_x(i):
+            a, e = HALF[i]
+            quant(xq, xs, xt, a, e)
+            if r == 3:
+                mm(P("psA", i, e - a), "qv", "sv", 0, xq, xs, a, e)
+                dma("y", "dout", T.oc[:, 4 * a:4 * e], T[xq][:, a:e].bitcast(dt.uint8), [(xq, a, e)], [])
+                for k in range(4):
+                    dma("s" if i and k > 1 else "y", "dout", T.osc[4 * k:4 * k + 4, a:e], T[xs][32 * k:32 * k + 4, a:e], [(xs, a, e)], [])
+                if i:
+                    vcopy(A("yo", a, e), P("psA", i, e - a))
+                else:
+                    act(A("yo", a, e), P("psA", i, e - a))
+                dma("s", "dout", T.y[:, a:e], T.yo[:, a:e], [("yo", a, e)], [])
+
         for i, (a, e) in enumerate(HALF):
             for b in range(4):
                 tt(strip(xt, b, a, e), ind(plane(hh, b), A(L, a // 16, e // 16)), plane(tb, b, a, e), ADD)
-            quant(xq, xs, xt, a, e)
-            if r == 3:
-                dma("y", "dout", T.oc[:, 4 * a:4 * e], T[xq][:, a:e].bitcast(dt.uint8), [(xq, a, e)], [])
-                for k in range(4):
-                    dma("y", "dout", T.osc[4 * k:4 * k + 4, a:e], T[xs][32 * k:32 * k + 4, a:e], [(xs, a, e)], [])
-                mm(P("psA", i, e - a), "qv", "sv", 0, xq, xs, a, e)
-                act(A("yo", a, e), P("psA", i, e - a))
-                dma("s", "dout", T.y[:, a:e], T.yo[:, a:e], [("yo", a, e)], [])
+                if (i, b) == (1, 0):
+                    pack_x(0)
+        if r < 3:
+            settle("hm_%d" % (r + 1), "hs_%d" % (r + 1))
+        pack_x(1)
         if r < 3:
             send_state(r + 1, MASKS[r])
             scores(r + 1)
             unpack("psA", xq, xs)
-            settle("hm_%d" % (r + 1), "hs_%d" % (r + 1))
             tt(N("rf", "dG_%d" % (r + 1)), ends("rb", "hs_%d" % (r + 1)), nf("rH"), SUB)
 
     for sem in sorted(total):

from concourse.mybir import dt, AluOpType, AxisListType, ActivationFunctionType

ADD, SUB, MUL, MAX = AluOpType.add, AluOpType.subtract, AluOpType.mult, AluOpType.max
GT, EQ, NE = AluOpType.is_gt, AluOpType.is_equal, AluOpType.not_equal
COPY, IDENT = ActivationFunctionType.Copy, ActivationFunctionType.Identity
C = 416
K = C // 16
MASKS = [1, 2, 3]
HALF = [(0, 288), (288, 416)]
CHUNK = [(4, 0, 16, 16), (5, 0, 32, 32), (6, 0, 64, 64), (7, 0, 128, 128), (7, 128, 256, 256), (7, 256, 288, 384)]


def layout(items):
    at, n = {}, 0
    for name, w in items:
        at[name] = (n, w)
        n += (w + 15) // 16 * 16
    return at, n


_rb = [(k, C) for k in ("mask", "hm", "cx", "one", "two", "iota", "t16", "om", "os", "W0")]
_rb += [("%s%d" % (k, s), C) for s in range(1, 8) for k in "WMS"]
_rb += [("mb%d" % s, 16) for s in range(4)] + [("og%d" % s, 16) for s in range(4)] + [("ds%d" % s, 16) for s in range(4)] + [("cp", 16)]
_rb += [("%s_%d" % (k, r), 432) for r in (1, 2, 3) for k in ("up", "sg", "g", "l", "ls", "so", "go", "PB", "pm", "ps", "OB", "am", "as", "rR", "hm", "hs")]
RB, NRB = layout(_rb)
_ru = [("G%d" % s, K) for s in range(1, 8)] + [("OG0", K), ("pick", 8)] + [("q%d" % s, 1) for s in range(5)]
_ru += [("%s_%d" % (k, r), K) for r in (1, 2, 3) for k in ("x", "sc", "ai", "bi", "og")]
RU, NRU = layout(_ru)
_rf = [(k, C) for k in ("i1024", "w0", "w0s", "rr", "rrs", "hf", "hfs", "nr")]
_rf += [("p16", 1), ("pw", 16), ("bit", 4), ("f0", 1), ("rG0", K), ("hd", K)] + [("fo%d" % s, 16) for s in range(4)]
_rf += [("%s_%d" % (k, r), C) for r in (1, 2, 3) for k in ("bf", "bs", "of", "os")]
_rf += [("%s_%d" % (k, r), K) for r in (1, 2, 3) for k in ("t2", "t3", "lG", "rG", "rH", "dG")]
RF, NRF = layout(_rf)
RI, NRI = layout([("nx", K), ("p", 1), ("p16", 1), ("bit", 4), ("pick", 8)])
WHERE = {"rb": RB, "ru": RU, "rf": RF, "ri": RI}

X4, U8, BF = "float8_e4m3fn_x4", "uint8", "bfloat16"
SCRATCH = {
    "rb": ("sbuf", [128, NRB], BF), "ru": ("sbuf", [128, NRU], "uint16"), "rf": ("sbuf", [128, NRF], "float32"), "ri": ("sbuf", [128, NRI], "int32"),
    "et": ("sbuf", [128, 528], BF), "qe": ("sbuf", [128, 512], X4), "se": ("sbuf", [128, 512], U8),
    "uin": ("sbuf", [128, 512], BF), "qu": ("sbuf", [128, 128], X4), "su": ("sbuf", [128, 128], U8),
    "u2": ("sbuf", [128, 128], X4), "s2": ("sbuf", [128, 128], U8),
    "vin": ("sbuf", [128, 512], BF), "qv": ("sbuf", [128, 128], X4), "sv": ("sbuf", [128, 128], U8),
    "wq": ("sbuf", [128, 512], X4), "wp": ("sbuf", [128, 512], U8),
    "yo": ("sbuf", [128, C], "float32"),
    "psA": ("psum", [128, 2048], "float32"), "psB": ("psum", [128, 2048], "float32"),
    "L0": ("sbuf", [128, 2 * K], "uint16"),
    "xt0": ("sbuf", [128, 4 * C], BF), "xq0": ("sbuf", [128, C], X4), "xs0": ("sbuf", [128, C], U8),
}
for _r in (1, 2, 3):
    for _n in ("th", "tp", "za", "zt", "hh", "tb", "xt"):
        SCRATCH["%s%d" % (_n, _r)] = ("sbuf", [128, 4 * C], BF)
    for _n in ("xq", "lq", "zq"):
        SCRATCH["%s%d" % (_n, _r)] = ("sbuf", [128, C], X4)
    for _n in ("xs", "lp", "zs"):
        SCRATCH["%s%d" % (_n, _r)] = ("sbuf", [128, C], U8)
    for _n in ("L", "LN", "LZ"):
        SCRATCH["%s%d" % (_n, _r)] = ("sbuf", [128, 2 * K], "uint16")
SEMAPHORES = ["cv", "cs", "ct", "cg", "dnx", "dx", "du", "dv", "dwc", "dws", "dout", "lsem"] + ["%s%d" % (k, r) for r in (1, 2, 3) for k in ("aN", "aZ", "aQ")]


def rank_program(g, core, T, topo):
    rank = T.rank_of(core)
    if rank is None:
        return
    eng = {"v": g.vector, "s": g.scalar, "t": g.tensor, "g": g, "y": g.sync}
    known = {q: {} for q in eng}
    count = {q: 0 for q in eng}
    clocks, wr, rd, total = {}, {}, {}, {}

    def over(a, b):
        return a[1] < b[2] and b[1] < a[2]

    def learn(q, sem, n):
        for k, v in list(clocks.get((sem, n), {}).items()) + [(sem, n)]:
            if known[q].get(k, 0) < v:
                known[q][k] = v

    def sync(q, reads, writes):
        need = {}
        for r in reads:
            for reg, ev in wr.get(r[0], []):
                if over(reg, r):
                    need[ev] = 1
            if r[0][:2] == "ps":
                for reg, ev in rd.get(r[0], []):
                    if over(reg, r) and ev[0] != "c" + q:
                        need[ev] = 1
        for w in writes:
            for reg, ev in wr.get(w[0], []) + rd.get(w[0], []):
                if over(reg, w):
                    need[ev] = 1
        for sem, n in sorted(need, key=lambda e: -len(clocks.get(e, {})) * 100000 - e[1]):
            if known[q].get(sem, 0) < n:
                eng[q].wait_ge(T.sem[sem], n)
                learn(q, sem, n)

    def mark(ev, q, reads, writes):
        clocks[ev] = dict(known[q]) if q else {}
        for w in writes:
            wr[w[0]] = [e for e in wr.get(w[0], []) if not (w[1] <= e[0][1] and e[0][2] <= w[2])] + [(w, ev)]
            rd[w[0]] = [e for e in rd.get(w[0], []) if not (w[1] <= e[0][1] and e[0][2] <= w[2])]
        for r in reads:
            rd.setdefault(r[0], []).append((r, ev))

    def op(q, f, reads, writes):
        sync(q, reads, writes)
        count[q] += 1
        sem = "c" + q
        f().then_inc(T.sem[sem], 1)
        total[sem] = count[q]
        mark((sem, count[q]), q, reads, writes)

    def dma(q, sem, out, in_, reads, writes):
        sync(q, reads, writes)
        eng[q].dma_start(out, in_).then_inc(T.sem[sem], 16)
        total[sem] = total.get(sem, 0) + 16
        mark((sem, total[sem]), q, reads, writes)

    def A(buf, a, b, step=1):
        return (T[buf][:, a:b] if step == 1 else T[buf][:, a:b:step], [(buf, a, b)])

    def N(buf, name, a=0, b=None):
        o, w = WHERE[buf][name]
        return A(buf, o + a, o + (w if b is None else b))

    def ends(buf, name, n=C):
        o = WHERE[buf][name][0]
        return A(buf, o + 15, o + n, 16)

    def ind(w, o):
        return (w[0].indirect(o[0]), w[1] + o[1])

    def P(buf, bank, n):
        return (T[buf][:, 512 * bank:512 * bank + n], [(buf, 512 * bank, 512 * bank + 512)])

    def plane(buf, b, a=0, e=C):
        return A(buf, C * b + a, C * b + e)

    def strip(buf, b, a, e):
        return (T[buf][:, 4 * a + b:4 * e:4], [("%s#%d" % (buf, b), a, e)])

    def tt(out, a, b, o):
        op("v", lambda: g.vector.tensor_tensor(out[0], a[0], b[0], o), a[1] + b[1], out[1])

    def ts(out, a, s1, o1, s2=None, o2=None):
        regs = list(a[1])
        if isinstance(s1, tuple):
            regs += s1[1]
            s1 = s1[0]
        if isinstance(s2, tuple):
            regs += s2[1]
            s2 = s2[0]
        if o2 is None:
            op("v", lambda: g.vector.tensor_scalar(out[0], a[0], s1, None, o1), regs, out[1])
        else:
            op("v", lambda: g.vector.tensor_scalar(out[0], a[0], s1, s2, o1, o2), regs, out[1])

    def vcopy(out, a):
        op("v", lambda: g.vector.tensor_copy(out[0], a[0]), a[1], out[1])

    def act(out, a, scale=1.0, bias=0.0):
        if bias == 0.0 and scale == 1.0:
            op("s", lambda: g.scalar.activation(out[0], a[0], COPY), a[1], out[1])
        else:
            op("s", lambda: g.scalar.activation(out[0], a[0], IDENT, bias=bias, scale=scale), a[1], out[1])

    def scan(out, a, b, init, o1, o2):
        regs = a[1] + b[1]
        if isinstance(init, tuple):
            regs = regs + init[1]
            init = init[0]
        op("v", lambda: g.vector.tensor_tensor_scan(out[0], a[0], b[0], init, o1, o2), regs, out[1])

    def memset(out, v):
        op("v", lambda: g.vector.memset(out[0], v), [], out[1])

    def iota(out, pattern, base, cm):
        op("g", lambda: g.iota(out[0], pattern, base, cm, allow_small_or_imprecise_dtypes=True), [], out[1])

    def quant(q, s, tile, a, e, t0=None):
        regs = [("%s#%d" % (tile, b), a, e) for b in range(4)] if t0 is None else [(tile, t0, t0 + 4 * (e - a))]
        i0 = 4 * a if t0 is None else t0
        op("v", lambda: g.vector.quantize_mx(T[q][:, a:e], T[s][:, a:e], T[tile][:, i0:i0 + 4 * (e - a)]), regs, [(q, a, e), (s, a, e)])

    def mm(out, lq, ls, la, rq, rs, a, e):
        op("t", lambda: g.tensor.matmul_mx(out[0], T[lq][:, la:la + 128], T[ls][:, la:la + 128], T[rq][:, a:e], T[rs][:, a:e], True, True),
           [(lq, la, la + 128), (ls, la, la + 128), (rq, a, e), (rs, a, e)], out[1])

    def peer(m):
        return T.cores[rank ^ m]

    def send(dst, sem, pairs, regs):
        rid, pid = topo.addr(dst)[:2]
        mask = topo.mask(core, dst)
        n = len(topo.engines(core, dst))
        sync("g", regs, [])
        for out, in_ in pairs:
            g.remote_dma(out, in_, T.sem[sem], T.sem.lsem, pid, rid, mask)
            total["lsem"] = total.get("lsem", 0) + n

    def arrives(src, sem, k, regs):
        n = k * len(topo.engines(src, core))
        total[sem] = n
        mark((sem, n), None, [], regs)

    def send_lists(src, dst_buf, sem, m):
        send(peer(m), sem, [(T[dst_buf][:, 0:2 * K], T[src][:, 0:2 * K])], [(src, 0, 2 * K)])
        arrives(peer(m), sem, 1, [(dst_buf, 0, 2 * K)])

    def send_state(r, m):
        xq, xs, lq, lp = "xq%d" % (r - 1), "xs%d" % (r - 1), "lq%d" % r, "lp%d" % r
        send(peer(m), "aQ%d" % r, [(T[lq][:, 0:C].bitcast(dt.uint8), T[xq][:, 0:C].bitcast(dt.uint8)), (T[lp][:, 0:C], T[xs][:, 0:C])], [(xq, 0, C), (xs, 0, C)])
        arrives(peer(m), "aQ%d" % r, 2, [(lq, 0, C), (lp, 0, C)])

    def scores(r):
        for i, (a, e) in enumerate(HALF):
            for k in (0, 2):
                mm(P("psB", i + k, e - a), "u2", "s2", 0, "xq%d" % (r - 1), "xs%d" % (r - 1), a, e)

    def unpack(ps, q, s):
        for b in range(4):
            mm(P(ps, b, C), "qe", "se", 128 * b, q, s, 0, C)

    def halves(ps, dst):
        for b in range(4):
            act(plane(dst, b), P(ps, b, C), scale=0.5)

    mask, hm, io = N("rb", "mask"), N("rb", "hm"), N("rb", "iota")

    def settle(m, s, n=C):
        scan(N("rb", s, 0, n), N("rb", "hm", 0, n), N("rb", m, 0, n), 0.0, MUL, ADD)

    def settle_max(*jobs):
        for buf, src, dst, out, shift in jobs:
            hold(buf, src, dst)
        for buf, src, dst, out, shift in jobs:
            ts(out, ends(buf, dst), N("rf", "pw", 15, 16), MUL, shift, ADD)

    def hold(buf, src, dst):
        scan(N(buf, dst, 0, C), N("rb", "cx"), N(buf, src, 0, C), 0.0, MUL, MAX)

    dma("y", "dnx", N("ri", "nx")[0], T.nx[:], [], N("ri", "nx")[1])
    dma("s", "dx", T.xt0[:], T.x[:], [], [("xt0", 0, 4 * C)])
    dma("y", "du", T.uin[:], T.u[:], [], [("uin", 0, 512)])
    dma("y", "dwc", T.wq[:].bitcast(dt.uint8), T.wc[:], [], [("wq", 0, 512)])
    dma("y", "dws", T.wp[:], T.ws[:], [], [("wp", 0, 512)])
    dma("y", "dv", T.vin[:], T.v[:], [], [("vin", 0, 512)])

    op("g", lambda: g.iota(N("ri", "p")[0], [[0, 1]], 0, 1), [], N("ri", "p")[1])
    iota(N("rb", "t16"), [[0, K], [1, 16]], 0, 0)
    op("g", lambda: g.iota(N("ri", "pick")[0], [[16, 8]], 0, 0), [], N("ri", "pick")[1])
    memset(N("rb", "one"), 1.0)
    memset(N("rf", "f0"), -208.0)
    memset(N("ru", "q0"), 0)
    scan(N("rf", "i1024"), N("rb", "one"), N("rb", "one"), 1023.0, MUL, ADD)
    act(io, N("rf", "i1024"), bias=-1232.0)
    act(N("rb", "two"), N("rb", "one"), scale=2.0)
    ts(N("ri", "p16"), N("ri", "p"), 15, AluOpType.bitwise_and)
    for s in range(4):
        ts(N("ri", "bit", s, s + 1), N("ri", "p"), s, AluOpType.logical_shift_right, 1, AluOpType.bitwise_and)
    vcopy(N("rf", "p16"), N("ri", "p16"))
    vcopy(N("rf", "bit"), N("ri", "bit"))
    vcopy(N("ru", "pick"), N("ri", "pick"))
    ts(N("rb", "mask"), N("rb", "t16"), N("rf", "p16"), EQ)
    ts(N("rb", "cp"), N("rb", "t16", 0, 16), N("rf", "p16"), GT, 0.5, MUL)
    act(hm, N("rb", "mask"), scale=-1.0, bias=1.0)
    ts(N("rb", "cx"), N("rb", "t16"), N("rf", "p16"), GT, 2.0, MUL)
    scan(N("rf", "pw"), N("rb", "cp"), N("rb", "mask", 0, 16), 0.0, MUL, ADD)
    for s in range(4):
        act(N("rb", "ds%d" % s), N("rb", "one", 0, 16))

    vcopy(A("L0", 0, K), N("ri", "nx"))
    w0 = N("rf", "w0")
    op("v", lambda: g.vector.tensor_copy(w0[0].indirect(T.L0[:, 0:K]), N("rf", "i1024")[0]), N("rf", "i1024")[1] + [("L0", 0, K)], w0[1])
    act(N("rb", "W0"), w0, bias=-1232.0)
    hold("rf", "w0", "w0s")
    for s in range(4):
        ts(N("rb", "mb%d" % s), N("rb", "mask", 0, 16), N("rf", "bit", s, s + 1), MUL)
    ts(A("L0", K, 2 * K), ends("rf", "w0s"), N("rf", "pw", 15, 16), MUL, -1024.0, ADD)
    for s in range(4):
        ts(N("rb", "ds%d" % s, 0, 1), N("rf", "bit", s, s + 1), -1.0, MUL, 1.0, ADD)
    memset(A("et", 0, 515), 1.0)
    op("g", lambda: g.affine_select(T.et[:, 0:515], T.et[:, 0:515], [[1, 515]], EQ, 0.0, -3, -4), [("et", 0, 515)], [("et", 0, 515)])
    send_lists("L0", "LN1", "aN1", MASKS[0])

    def first_x():
        quant("xq0", "xs0", "xt0", 0, C, 0)
        send_state(1, MASKS[0])

    def first_u():
        quant("qu", "su", "uin", 0, 128, 0)
        pk = N("ru", "pick")
        op("v", lambda: g.vector.tensor_copy(T.u2[:, 0:128].bitcast(dt.uint32), T.qu[:, 0:128].bitcast(dt.uint32).indirect(pk[0])), [("qu", 0, 128)] + pk[1], [("u2", 0, 128)])
        op("s", lambda: g.scalar.activation(T.s2[:, 0:128], T.su[:, 0:128].indirect(pk[0]), COPY), [("su", 0, 128)] + pk[1], [("s2", 0, 128)])

    def constant(b):
        op("v", lambda: g.vector.quantize_mx(T.qe[:, 128 * b:128 * b + 128], T.se[:, 128 * b:128 * b + 128], T.et[:, 3 - b:515 - b]), [("et", 0, 515)], [("qe", 128 * b, 128 * b + 128), ("se", 128 * b, 128 * b + 128)])

    def up(r, i):
        a, e = HALF[i]
        ts(N("rb", "up_%d" % r, a, e), P("psB", i + 2, e - a), 0.0, GT)
        out, ps = N("rb", "sg_%d" % r, a, e), P("psB", i, e - a)
        op("s", lambda: g.scalar.activation(out[0], ps[0], ActivationFunctionType.Sign), ps[1], out[1])

    def chunk(c, part):
        s, a, e, to = CHUNK[c]
        n = e - a
        if part == 0:
            tt(N("rb", "om", to, to + n), ind(N("rb", "W%d" % s), N("ru", "OG0", a // 16, e // 16) if c else N("ru", "q4")), N("rb", "mask", 0, n), MUL)
        if part == 1:
            scan(N("rb", "os", to, to + n), N("rb", "hm", 0, n), N("rb", "om", to, to + n), 0.0, MUL, ADD)
        if part == 2:
            o = RB["os"][0]
            ts(N("ru", "OG0", to // 16, to // 16 + n // 16), A("rb", o + to + 15, o + to + n, 16), 208.0, ADD)

    for s in range(5):
        src = A("L0", K, 2 * K) if s == 0 else N("ru", "G%d" % s)
        w = N("rb", "W%d" % s)
        small = s < 4
        act(N("rb", "W%d" % (s + 1)), ind(w, src))
        tt(N("rb", "M%d" % s if s else "om"), ind(w, src), mask, MUL)
        if small:
            tt(N("rb", "og%d" % s), ind(w, N("ru", "q%d" % s)), N("rb", "mb%d" % s), MUL)
        else:
            chunk(s - 4, 0)
        if s:
            settle("M%d" % s, "S%d" % s)
        else:
            settle("om", "os")
        if small:
            scan(N("rf", "fo%d" % s), N("rb", "ds%d" % s), N("rb", "og%d" % s), N("rf", "fo%d" % (s - 1), 15, 16) if s else N("rf", "f0"), MUL, ADD)
        else:
            chunk(s - 4, 1)
        ts(N("ru", "G%d" % (s + 1)), ends("rb", "S%d" % s if s else "os"), 208.0, ADD)
        if small:
            ts(N("ru", "q%d" % (s + 1)), N("rf", "fo%d" % s, 15, 16), 208.0, ADD)
            if s == 3:
                vcopy(N("ru", "OG0", 0, 1), N("ru", "q4"))
        else:
            chunk(s - 4, 2)
    act(N("rb", "W6"), ind(N("rb", "W5"), N("ru", "G5")))
    act(N("rb", "M7"), ind(N("rb", "W6"), N("ru", "G5")))
    act(N("rb", "W7"), ind(N("rb", "M7"), N("ru", "G5")))
    for part in range(3):
        chunk(1, part)
    first_x()
    for part in range(3):
        chunk(2, part)
    first_u()
    scores(1)
    for c in (3, 4, 5):
        for part in range(3):
            chunk(c, part)
            if c < 5 and part < 2:
                constant(2 * c - 6 + part)
            if c == 5 and part < 2:
                up(1, part)
    unpack("psA", "xq0", "xs0")
    rr = N("rf", "rr")
    order = N("ru", "OG0")
    op("v", lambda: g.vector.tensor_copy(rr[0].indirect(order[0]), N("rf", "i1024")[0]), N("rf", "i1024")[1] + order[1], rr[1])
    act(N("rf", "hf"), ind(rr, A("LN1", K, 2 * K)))
    rG = N("rf", "rG0")
    hold("rf", "rr", "rrs")


    for r in (1, 2, 3):
        m = MASKS[r - 1]
        L, LN, LZ = "L%d" % r, "LN%d" % r, "LZ%d" % r
        nb = lambda k, a=0, b=C: N("rb", "%s_%d" % (k, r), a, b)
        nu = lambda k: N("ru", "%s_%d" % (k, r))
        nf = lambda k: N("rf", "%s_%d" % (k, r))
        if r > 1:
            up(r, 0)
            up(r, 1)
        tt(nb("g"), ind(nb("sg"), A(LN, 0, K)), nb("up"), GT)
        act(nb("go"), ind(nb("g"), order))
        if r == 1:
            ts(rG, ends("rf", "rrs"), N("rf", "pw", 15, 16), MUL, -1231.0, ADD)
        tt(nb("l"), ind(nb("g"), A(LN, K, 2 * K)), N("rb", "two"), ADD)
        act(nb("so"), ind(nb("l"), order), scale=-1.0, bias=3.0)
        lG = nf("lG")
        left = ("rb", "l_%d" % r, "ls_%d" % r, lG, -2.0)
        if r == 1:
            settle_max(left, ("rf", "hf", "hfs", N("rf", "hd"), -1231.0))
            tt(nf("dG"), N("rf", "hd"), rG, SUB)
        else:
            settle_max(left)
        tt(nf("t2"), lG, nf("dG"), MUL)
        tt(nf("t3"), nf("t2"), rG, ADD)
        ts(nu("x"), nf("t3"), 207.0, ADD)
        scan(nb("PB", 0, C), nb("so"), nb("go"), -208.0, ADD, ADD)
        halves("psA", "th%d" % r)
        if r == 1:
            unpack("psB", "lq1", "lp1")
            halves("psB", "tp1")
        tt(nb("pm"), ind(nb("PB"), nu("x")), mask, MUL)
        settle("pm_%d" % r, "ps_%d" % r)
        tt(nf("rG"), ends("rb", "ps_%d" % r), lG, SUB)
        rG = nf("rG")
        ts(nu("sc"), rG, 208.0, ADD)
        ts(nu("ai"), rG, 207.0, ADD)
        ts(nu("bi"), rG, 209.0, ADD)
        ob = nb("OB", 0, 417)
        op("v", lambda: g.vector.tensor_copy(ob[0].indirect(nu("sc")[0]), io[0]), io[1] + nu("sc")[1], ob[1])
        vcopy(nb("OB", 0, 1), nb("OB", 416, 417))
        act(nb("OB", 417, 418), nb("OB", 1, 2))
        tt(nb("am"), ind(nb("OB"), nu("ai")), mask, MUL)
        act(nf("bf"), ind(nb("OB", 0, 418), nu("bi")), bias=1232.0)
        settle("am_%d" % r, "as_%d" % r)
        hold("rf", "bf_%d" % r, "bs_%d" % r)
        ts(A(L, 0, K), ends("rb", "as_%d" % r), 208.0, ADD)
        ts(A(L, K, 2 * K), ends("rf", "bs_%d" % r), N("rf", "pw", 15, 16), MUL, -1024.0, ADD)
        send_lists(L, LZ, "aZ%d" % r, m)
        if r < 3:
            send_lists(L, "LN%d" % (r + 1), "aN%d" % (r + 1), MASKS[r])
            act(nf("of"), nb("OB", 1, 417), bias=1232.0)
            rr = nb("rR")
            tt(rr, ind(nb("PB"), nu("x")), nb("l", 0, C), SUB)
            ts(nf("rH"), rG, -2.0, ADD)
            settle_max(("rf", "of_%d" % r, "os_%d" % r, nu("og"), -1024.0))
            order = nu("og")
        if r == 1:
            quant("qv", "sv", "vin", 0, 128, 0)
        else:
            unpack("psB", "lq%d" % r, "lp%d" % r)
            halves("psB", "tp%d" % r)
        th, tp, tb, za, zt, hh, xt = ["%s%d" % (k, r) for k in ("th", "tp", "tb", "za", "zt", "hh", "xt")]
        zq, zs, xq, xs = ["%s%d" % (k, r) for k in ("zq", "zs", "xq", "xs")]

        for b in range(4):
            if b in ((3,), (1, 2), (1, 2, 3))[r - 1]:
                vcopy(plane(tb, b), ind(plane(th, b), A(L, K, 2 * K)))
            elif (r, b) != (2, 3):
                act(plane(tb, b), ind(plane(th, b), A(L, K, 2 * K)))
        def pack_z(i):
            a, e = HALF[i]
            quant(zq, zs, zt, a, e)
            for b in range(4):
                mm(P("psB" if i else "psA", b, e - a), "wq", "wp", 128 * b, zq, zs, a, e)

        for i, (a, e) in enumerate(HALF):
            for b in range(4):
                for a1, e1 in ((a, a + 96), (a + 96, e)) if (i, b) == (0, 0) else ((a, e),):
                    act(plane(za, b, a1, e1), ind(plane(tp, b), A(LZ, a1 // 16, e1 // 16)))
                    tt(strip(zt, b, a1, e1), ind(plane(tp, b), A(LZ, K + a1 // 16, K + e1 // 16)), plane(za, b, a1, e1), ADD)
                if (i, b) == (1, 0):
                    pack_z(0)
        pack_z(1)
        if r < 3:
            tt(N("rb", "hm_%d" % (r + 1), 0, C), ind(rr, A("LN%d" % (r + 1), K, 2 * K)), mask, MUL)
        a, e = HALF[0]
        for b in range(4):
            act(plane(hh, b, a, e), P("psA", b, e - a), scale=0.015625)
        a, e = HALF[1]
        for b in range(4):
            if b % 2:
                act(plane(hh, b, a, e), P("psB", b, e - a), scale=0.015625)
            else:
                ts(plane(hh, b, a, e), P("psB", b, e - a), 0.015625, MUL)
        if r == 2:
            act(plane(tb, 3), ind(plane(th, 3), A(L, K, 2 * K)))
        if r == 3:
            act(N("rf", "nr"), ind(nb("OB"), nu("ai")), bias=208.0)
            dma("y", "dout", T.nr[:, :], T.rf[0:128:16, RF["nr"][0]:RF["nr"][0] + C], N("rf", "nr")[1], [])
        def pack_x(i):
            a, e = HALF[i]
            quant(xq, xs, xt, a, e)
            if r == 3:
                mm(P("psA", i, e - a), "qv", "sv", 0, xq, xs, a, e)
                dma("y", "dout", T.oc[:, 4 * a:4 * e], T[xq][:, a:e].bitcast(dt.uint8), [(xq, a, e)], [])
                for k in range(4):
                    dma("s" if i and k > 1 else "y", "dout", T.osc[4 * k:4 * k + 4, a:e], T[xs][32 * k:32 * k + 4, a:e], [(xs, a, e)], [])
                if i:
                    vcopy(A("yo", a, e), P("psA", i, e - a))
                else:
                    act(A("yo", a, e), P("psA", i, e - a))
                dma("s", "dout", T.y[:, a:e], T.yo[:, a:e], [("yo", a, e)], [])

        for i, (a, e) in enumerate(HALF):
            for b in range(4):
                tt(strip(xt, b, a, e), ind(plane(hh, b), A(L, a // 16, e // 16)), plane(tb, b, a, e), ADD)
                if (i, b) == (1, 0):
                    pack_x(0)
        if r < 3:
            settle("hm_%d" % (r + 1), "hs_%d" % (r + 1))
        pack_x(1)
        if r < 3:
            send_state(r + 1, MASKS[r])
            scores(r + 1)
            unpack("psA", xq, xs)
            tt(N("rf", "dG_%d" % (r + 1)), ends("rb", "hs_%d" % (r + 1)), nf("rH"), SUB)

    for sem in sorted(total):
        g.wait_ge(T.sem[sem], total[sem])
